import numpy as np, ml_dtypes
CORES = [5,29,101,125,133,157,229,253]
N = 8
BF = ml_dtypes.bfloat16
def gentries(a):
    return np.ascontiguousarray(a.reshape(8, 16, -1).transpose(0, 2, 1)).reshape(8, -1)
def gtable(e):
    e = np.asarray(e); return np.ascontiguousarray(e.reshape(8, -1, 16).transpose(0, 2, 1)).reshape(128, -1).astype(np.int32)
L, CAP, S, RO, PA = 1024, 192, 64, 2, 2
V = L + RO * CAP; W = V + (N - 1) * 2 * S + 1; NONE = W - 1
G8 = np.arange(8)[:, None]
ARR = np.concatenate([V + (d - 1) * 2 * S + np.arange(S) for d in range(1, N)])
def columns(x):
    return np.ascontiguousarray(x.reshape(N, 8, 16, -1).transpose(0, 1, 3, 2))
def flat(x):
    return np.ascontiguousarray(x.transpose(0, 1, 3, 2)).reshape(N, 128, -1)
def slots(rng, n, share):
    e = rng.integers(0, L, (N, 8, L, 16)); far = ARR[rng.integers(0, len(ARR), e.shape)]
    e = np.where(rng.random(e.shape) < share, far, e)
    return np.where(np.argsort(rng.random(e.shape), axis=-1) < n, e, NONE)
def showing(rng):
    return np.ascontiguousarray(np.argsort(rng.random((N, 8, N - 1, L)), axis=-1)[..., :S])
def pack(e, v, th, sh):
    return {"e": flat(e).astype(np.int32), "v0": flat(v).astype(np.float32).astype(BF), "th": np.ascontiguousarray(np.repeat(th, 16, axis=1)[:, :, None]).astype(np.int32),
            "sh": np.stack([gtable(a.reshape(8, -1)) for a in sh])}
def setup_inputs(rng):
    e = slots(rng, rng.integers(6, 17, (N, 8, L, 1)), 0.3)
    v = (256 * (0.25 + 0.75 * rng.random((N, 8, L, 1))) * rng.random((N, 8, L, 16))).astype(np.int64)
    base = np.array([120, 250, 400, 550, 700, 900, 1100, 1400])
    th = base[np.argsort(rng.random((N, 8)), axis=1)] + rng.integers(-50, 51, (N, 8))
    return pack(e, v, th, showing(rng))
def setup_inputs_room(rng):
    e = slots(rng, rng.integers(15, 17, (N, 8, L, 1)), 0.3)
    n = rng.choice(np.array([0, 1, CAP - 1, CAP, CAP + 1, L]), (N, 8)); n[0] = [CAP, CAP + 1, L, CAP - 1, 1, 0, CAP, CAP + 1]
    hot = np.argsort(rng.random((N, 8, L)), axis=-1) < n[:, :, None]; hot[0, 4] = False; hot[0, 4, L - 1] = True
    v = np.where(hot[..., None], rng.integers(200, 256, (N, 8, L, 16)), rng.integers(136, 200, (N, 8, L, 16)))
    return pack(e, v, np.full((N, 8), 3200), showing(rng))
def setup_inputs_ties(rng):
    e = slots(rng, rng.choice(np.array([8, 10, 12, 16]), (N, 8, L, 1)), 0.3)
    base = rng.integers(8, 128, (1, 8, 1, 16)); kind = rng.integers(1, 3, (N, 8, L, 1)); kind[:, ::2] = 2
    add = rng.integers(0, 2, (N, 8)); add[0] = 0; add[1, ::2] = 1
    th = np.sum(base, axis=-1)[..., 0] * np.where(np.arange(8) % 2 == 0, 2, 1)[None, :] + add
    return pack(e, base * kind, th, showing(rng))
def setup_inputs_ends(rng):
    e = slots(rng, rng.integers(10, 17, (N, 8, L, 1)), 0.3); v = rng.integers(60, 256, (N, 8, L, 16)); sh = showing(rng)
    e[:, 0] = rng.choice(np.array([0, L - 1, L, V - 1, V, V + S - 1, V + S, W - 2, NONE]), (N, L, 16))
    e[:, 1] = rng.integers(0, W, (N, L, 16)); e[:, 2] = ARR[rng.integers(0, len(ARR), (N, L, 16))]; e[:, 3] = rng.integers(0, L, (N, L, 16))
    e[:, 4] = rng.integers(0, L, (N, L, 1)); e[:, 4, :, 9] = NONE
    e[:, 5] = np.where(rng.random((N, L, 1)) < 0.3, NONE, e[:, 5])
    sh[:, ::2] = rng.choice(np.array([0, L - 1, L >> 1, 3]), (N, 4, N - 1, S))
    th = rng.choice(np.array([1, 2, 500, 1500]), (N, 8)); th[0, 7] = 4096; th[1, 0] = 1
    return pack(e, v, th, sh)
def setup_inputs_heavy(rng):
    e = slots(rng, rng.integers(0, 4, (N, 8, L, 1)), 0.2); v = rng.integers(1, 32, (N, 8, L, 16))
    o = 8 + np.argsort(rng.random((N, 8, L - 8)), axis=-1)[..., :64]; kind = rng.integers(0, 4, (N, 8, L))
    a = np.take_along_axis(o, rng.integers(0, 64, (N, 8, L)), 2); b = np.take_along_axis(o, rng.integers(0, 64, (N, 8, L)), 2)
    e[..., 0] = np.where((kind == 0) | (kind == 3), a, e[..., 0]); e[..., 15] = np.where((kind == 1) | (kind == 3), b, e[..., 15])
    one = np.arange(16) == rng.integers(0, 16, (N, 8, L, 1))
    e = np.where(kind[..., None] == 2, np.where(one, a[..., None], NONE), e)
    for q in range(N):
        for g in range(8):
            e[q, g, o[q, g]] = rng.choice(o[q, g], (64, 16)); v[q, g, o[q, g]] = 255
    e[:, :, 0] = NONE; v[:, :, :PA + 1] = 200
    for j in range(1, PA + 1): e[:, :, j] = j - 1
    e[:, ::2, PA, 0] = NONE
    th = rng.choice(np.array([1, 150, 250, 4080]), (N, 8)); th[0, 0] = 150; th[1, 3] = 4080; th[2, 5] = 2040; th[3, 3] = 4081; th[:, 6:] = 1
    sh = showing(rng)
    e[:, 6, :, 8:] = np.arange(L)[None, :, None]; v[:, 6] = rng.integers(1, 256, (N, L, 16))
    at = 0
    for r in range(RO):
        m = at + PA * (r + 1); e[:, 6, at] = NONE; v[:, 6, at:m + 1] = 200
        for j in range(at + 1, m + 1): e[:, 6, j] = j - 1
        e[1::2, 6, m, 0] = NONE
        at = m + 1 + CAP
    e[:, 6, PA + 1] = PA + 3; e[:, 6, PA + 1, 0] = PA + 2; v[:, 6, PA + 2] = 250; v[:, 6, PA + 3] = 255
    v[:, 6, L - 16:] = 0; e[:, 6, L - 16:] = NONE; e[:, 6, L - 16:, 3] = PA + 4; e[:, 6, L - 32:L - 16, 5] = np.arange(L - 16, L)
    t0 = (RO - 1) * CAP + 1; pool = np.concatenate([t0 + np.arange(CAP - 1), ARR])
    e[:, 7] = pool[rng.integers(0, len(pool), (N, L, 16))]; e[:, 7, :, 5:11] = NONE
    v[:, 7] = rng.integers(1, 256, (N, L, 16)); v[:, 7, t0:t0 + CAP - 1] = rng.integers(204, 256, (N, CAP - 1, 16))
    sh[:, 7] = t0 + np.argsort(rng.random((N, N - 1, CAP - 1)), axis=-1)[..., :S]; sh[:, 7, 0] = t0 + rng.integers(0, CAP - 1, (N, 1))
    e[:, 7, 0, 0] = ARR[-1]; e[:, 7, 1, 0] = V + S - 1
    e[1, 7, L - 1] = NONE; v[1, 7, L - 1] = 255; sh[1, 7, 1, 0] = L - 1; e[3, 7, 2] = V + 2 * S; v[3, 7, 2] = 255
    return pack(e, v, th, sh)
def setup_inputs_spread(rng):
    e = slots(rng, 16 - (14 * rng.random((N, 8, L, 1)) ** 2).astype(np.int64), 0.3)
    e = np.where((e < L) & (rng.random(e.shape) < 0.7), (L * rng.random(e.shape) ** 3).astype(np.int64), e)
    v = np.minimum((np.exp2(3 + 5 * rng.random((N, 8, L, 1))) * rng.random((N, 8, L, 16))).astype(np.int64), 255)
    th = np.minimum(np.maximum(np.exp2(12 * rng.random((N, 8))).astype(np.int64), 1), 4096); th[:, 2] = np.minimum(th[:, 2], 30)
    return pack(e, v, th, showing(rng))
def check_inputs(d):
    bad = []
    for k, lo, hi in (("e", 0, W - 1), ("th", 1, 4096), ("sh", 0, L - 1)):
        if np.min(d[k]) < lo or np.max(d[k]) > hi: bad.append("range of " + k)
    x = np.asarray(d["v0"]).astype(np.float64)
    if not np.all((x >= 0) & (x <= 255) & (x == np.floor(x))): bad.append("v0 is not whole numbers from 0 to 255")
    t = np.asarray(d["th"]).reshape(N, 8, 16)
    if not np.all(t == t[:, :, :1]): bad.append("th differs inside a group")
    return bad
def reference(e, v0, th, sh):
    E = np.full((N, 8, V, 16), NONE, np.int32); E[:, :, :L] = columns(e)
    v = np.zeros((N, 8, V, 16), np.int32); v[:, :, :L] = columns(v0.astype(np.float32)).astype(np.int32)
    t = th.reshape(N, 8, 16)[:, :, 0].astype(np.int64)
    half = np.full((N, 8, L), V, np.int64)
    sl = np.stack([gentries(a) for a in sh]).astype(np.int64).reshape(N, 8, N - 1, S)
    def show():
        z = np.concatenate([v, np.zeros((N, 8, 1, 16), np.int32)], axis=2); w = np.zeros((N, 8, W, 16), np.int32); w[:, :, :V] = v
        for a in range(N):
            for d in range(1, N):
                q = (a - d) % N; ix = sl[q, :, d - 1]; b = V + (d - 1) * 2 * S
                w[a, :, b:b + S] = z[q][G8, ix]; w[a, :, b + S:b + 2 * S] = z[q][G8, half[q][G8, ix]]
        return w
    for rnd in range(RO):
        for step in range(PA):
            w = show()
            for a in range(N):
                for g in range(8):
                    v[a, g] = np.minimum(v[a, g], np.add.reduce(w[a, g][E[a, g]], axis=1) >> 3)
        w = show(); fresh = np.zeros((N, 8, L), bool); new = np.full((N, 8, W), -1, np.int32)
        for a in range(N):
            for g in range(8):
                s = np.flatnonzero((half[a, g] == V) & (np.add.reduce(v[a, g, :L], axis=1) >= t[a, g]))[:CAP]
                h = L + CAP * rnd + np.arange(len(s)); old = E[a, g, s]
                C = np.add.accumulate(np.add.reduce(w[a, g][old], axis=2), axis=1)
                cut = np.argmax(2 * C >= C[:, 15:], axis=1); behind = np.arange(16)[None, :] > cut[:, None]
                E[a, g, h] = np.where(behind, old, NONE); E[a, g, s] = np.where(behind, NONE, old)
                x = (v[a, g, s] + 1) >> 1; v[a, g, s] = x; v[a, g, h] = x
                half[a, g, s] = h; fresh[a, g, s] = True; new[a, g, s] = h
        for a in range(N):
            for d in range(1, N):
                q = (a - d) % N; ix = sl[q, :, d - 1]; b = V + (d - 1) * 2 * S
                new[a, :, b:b + S] = np.where(fresh[q][G8, ix], b + S + np.arange(S)[None, :], -1)
            for g in range(8):
                n = new[a, g][E[a, g]]; has = n >= 0; empty = E[a, g] == NONE
                i = np.argmax(has, axis=1); m = np.argmax(empty, axis=1); c = np.flatnonzero(np.any(has, axis=1) & np.any(empty, axis=1))
                E[a, g, c, m[c]] = n[c, i[c]]
    return {"ye": flat(E).astype(np.float32), "yv": flat(v).astype(np.float32).astype(BF)}

@@ -1,0 +1,689 @@
+from concourse.bass import DstId, RemoteDMATransfer
+from concourse.mybir import dt, AluOpType as A, ActivationFunctionType as F
+
+NA, OWN, WW = 896, 904, 2312
+L, CAP, S, V = 1024, 192, 64, 1408
+NP = 64
+Y1, Y2, Y3 = 2, 2, 2
+LAG = 2
+RING = 16
+WID = [64, 64, 64, 128, 128, 128, 64]
+MAGIC8 = 1572864.0
+
+SCRATCH = {
+    "shi": ("sbuf", [128, 28], "int32"), "thi": ("sbuf", [128, 1], "int32"), "e32": ("sbuf", [128, 1024], "int32"),
+    "shl": ("sbuf", [128, 28], "uint16"), "shm": ("sbuf", [128, 28], "uint16"), "sh56": ("sbuf", [128, 56], "uint16"),
+    "z": ("sbuf", [128, 384], "bfloat16"), "xa": ("sbuf", [128, 1024], "float32"),
+    "off": ("sbuf", [128, 1408], "uint16"), "ef": ("sbuf", [128, 1600], "float32"), "tf": ("sbuf", [128, 1024], "float32"),
+    "gr": ("sbuf", [128, RING * NP * 16], "bfloat16"), "ci": ("sbuf", [128, 1216], "int32"),
+    "thf": ("sbuf", [128, 1], "float32"),
+    "pc": ("sbuf", [128, 4], "int32"), "pf": ("sbuf", [128, 16], "float32"),
+    "mi": ("sbuf", [128, 128], "float32"), "mg": ("sbuf", [128, 128], "float32"), "mm": ("sbuf", [128, 128], "float32"),
+    "i16": ("sbuf", [128, 16], "float32"), "lfc": ("sbuf", [128, 16], "float32"), "tmpc": ("sbuf", [128, 128], "float32"),
+    "mats": ("sbuf", [128, 16 * 128], "bfloat16"), "cola": ("sbuf", [128, 2048], "bfloat16"),
+    "pfx": ("sbuf", [128, 2048], "bfloat16"), "lf": ("sbuf", [128, 2048], "float16"),
+    "cposn": ("sbuf", [128, 64], "float32"), "iotac": ("sbuf", [128, 1024], "float32"), "padj": ("sbuf", [128, 192], "float32"),
+    "c192": ("sbuf", [128, 1024], "bfloat16"), "cb1": ("sbuf", [128, 256], "bfloat16"), "cb2": ("sbuf", [128, 256], "bfloat16"),
+    "cb3": ("sbuf", [128, 256], "bfloat16"), "cm1": ("sbuf", [128, 256], "bfloat16"),
+    "cand": ("sbuf", [128, 1024], "bfloat16"), "p0": ("sbuf", [128, 1040], "bfloat16"), "p1": ("sbuf", [128, 1040], "bfloat16"),
+    "hp": ("sbuf", [128, 1024], "bfloat16"), "hb": ("sbuf", [128, 1216], "bfloat16"), "g2": ("sbuf", [128, 1024], "bfloat16"),
+    "xp": ("sbuf", [128, 1408], "bfloat16"), "hs": ("sbuf", [128, 448], "bfloat16"), "an": ("sbuf", [128, 448], "bfloat16"),
+    "la": ("sbuf", [128, 64], "float32"), "lb": ("sbuf", [128, 64], "float32"), "lc": ("sbuf", [128, 64], "float32"),
+    "pos": ("sbuf", [128, 64], "uint16"), "lst": ("sbuf", [128, 1216], "float32"), "l16": ("sbuf", [128, 192], "float16"),
+    "slist": ("sbuf", [128, 12], "uint16"), "old": ("sbuf", [128, 192], "float32"), "offo": ("sbuf", [128, 192], "uint16"),
+    "beh": ("sbuf", [128, 192], "float32"), "hm": ("sbuf", [128, 2120], "float32"), "hg": ("sbuf", [128, 448], "float16"),
+    "em": ("sbuf", [128, 1408], "bfloat16"), "fe": ("sbuf", [128, 1408], "bfloat16"),
+    "k8": ("sbuf", [128, 1216], "float32"), "ff": ("sbuf", [128, 1408], "bfloat16"), "fx": ("sbuf", [128, 1408], "float16"),
+    "tl": ("sbuf", [128, 76], "uint16"), "ab": ("sbuf", [128, 1216], "bfloat16"), "tin": ("sbuf", [128, 1216], "float32"),
+    "nm": ("sbuf", [128, 1408], "float32"), "zz": ("sbuf", [128, 1408], "float32"), "et": ("sbuf", [128, 1408], "float32"),
+    "nc": ("sbuf", [128, 1408], "float16"), "yeb": ("sbuf", [128, 1408], "float32"),
+    "cw": ("sbuf", [128, 1024], "bfloat16"), "sfl": ("sbuf", [128, 1024], "bfloat16"),
+}
+for _k in range(7):
+    SCRATCH["W%d" % _k] = ("sbuf", [128, WW], "bfloat16")
+    SCRATCH["snd%d" % _k] = ("sbuf", [128, 7 * WID[_k]], "bfloat16")
+    SCRATCH["rb%d" % _k] = ("sbuf", [128, 4 * WID[_k]], "bfloat16")
+for _k in range(8):
+    SCRATCH["ps%d" % _k] = ("psum", [128, 512], "float32")
+LOADS = ["ld_sh", "ld_th", "ld_v", "ld_e0", "ld_e1"]
+SEMAPHORES = (["qv", "qs", "qt", "qg", "lsem", "sty", "stv"] + LOADS + ["arr%d" % k for k in range(7)] + ["rl%d" % k for k in range(7)])
+
+
+def split_engines(engs, n):
+    c = 1
+    while c * 2 * n <= len(engs):
+        c *= 2
+    cnt = [c] * n
+    left = len(engs) - c * n
+    for i in range(n):
+        if left >= cnt[i]:
+            left -= cnt[i]
+            cnt[i] *= 2
+    out, at = [], 0
+    for x in cnt:
+        out.append(engs[at:at + x])
+        at += x
+    return out
+
+
+def bits(engs):
+    m = 0
+    for x in engs:
+        m |= 1 << x
+    return m
+
+
+def plan(core, T, topo):
+    n = len(T.cores)
+    me = T.rank_of(core)
+    dst = {d: T.cores[(me + d) % n] for d in range(1, n)}
+    far = [d for d in range(1, n) if not topo.may_write(core, dst[d])]
+    near = [d for d in range(1, n) if topo.may_write(core, dst[d])]
+    rel = [c for c in topo.cores_of(core) if c != core and all(topo.may_write(c, dst[d]) for d in far)]
+    rel = sorted(rel, key=lambda c: (topo.die(c) != topo.die(core), c))
+    hop = {d: rel[i % len(rel)] for i, d in enumerate(far)}
+    slot = {d: i // len(rel) for i, d in enumerate(far)}
+    e1 = split_engines(topo.engines(core, rel[0]), len(far))
+    e2 = split_engines(topo.engines(core, dst[near[0]]), len(near))
+    return {"dst": dst, "far": far, "near": near, "hop": hop, "slot": slot,
+            "eng": {**{d: e1[i] for i, d in enumerate(far)}, **{d: e2[i] for i, d in enumerate(near)}}}
+
+
+def relay_program(g, core, T, topo):
+    for src in T.cores:
+        if src in topo.cores_of(core):
+            p = plan(src, T, topo)
+            mine = [d for d in p["far"] if p["hop"][d] == core]
+            if not mine:
+                return
+            tot = 0
+            for k in range(7):
+                w = WID[k]
+                g.wait_ge(T.sem["rl%d" % k], sum(len(p["eng"][d]) for d in mine))
+                for d in mine:
+                    rid, pid = topo.addr(p["dst"][d], core)
+                    en = topo.engines(core, p["dst"][d])
+                    g.remote_dma(out_ap=T["W%d" % k][:, (d - 1) * 128:(d - 1) * 128 + w],
+                                 in_ap=T["rb%d" % k][:, p["slot"][d] * w:(p["slot"][d] + 1) * w],
+                                 remote_sem=T.sem["arr%d" % k], local_sem=T.sem.lsem, pid=pid, routing_id=rid, dma_engine_mask=bits(en))
+                    tot += len(en)
+            g.wait_ge(T.sem.lsem, tot)
+
+
+def rank_program(g, core, T, topo):
+    rank = T.rank_of(core)
+    if rank is None:
+        relay_program(g, core, T, topo)
+        return
+    p = plan(core, T, topo)
+    order = p["far"] + p["near"]
+    nfar = len(p["far"])
+    Q = {"v": g.vector, "s": g.scalar, "t": g.tensor, "g": g, "y": g.sync}
+    SEM = {"v": "qv", "s": "qs", "t": "qt", "g": "qg"}
+    cnt = {"v": 0, "s": 0, "t": 0, "g": 0}
+    clk = {e: {} for e in Q}
+    snaps = {}
+    acc = {}
+
+    def conflicts(e, R, W):
+        need = {}
+        for wr, regs in ((False, R), (True, W)):
+            for (b, lo, hi) in regs:
+                ps = b[:2] == "ps"
+                for (alo, ahi, ae, asem, an, aw) in acc.get(b, ()):
+                    if ahi <= lo or hi <= alo:
+                        continue
+                    if ps and ae == e == "t":
+                        continue
+                    if not (wr or aw) and (ae == e or not ps):
+                        continue
+                    if clk[e].get(asem, 0) < an:
+                        need[asem] = max(need.get(asem, 0), an)
+        return need
+
+    def waits(e, need):
+        todo = sorted(need.items())
+        drop = set()
+        for (s, n) in todo:
+            for (s2, n2) in todo:
+                if s2 != s and s2 not in drop and snaps.get((s2, n2), {}).get(s, 0) >= n:
+                    drop.add(s)
+        for (s, n) in todo:
+            if s in drop:
+                continue
+            Q[e].wait_ge(T.sem[s], n)
+            clk[e][s] = max(clk[e].get(s, 0), n)
+            for k2, v2 in snaps.get((s, n), {}).items():
+                if clk[e].get(k2, 0) < v2:
+                    clk[e][k2] = v2
+
+    def note(e, sem, n, R, W):
+        for wr, regs in ((False, R), (True, W)):
+            for (b, lo, hi) in regs:
+                lst = acc.setdefault(b, [])
+                if wr:
+                    lst[:] = [a for a in lst if not (a[0] >= lo and a[1] <= hi)]
+                else:
+                    lst[:] = [a for a in lst if not (a[0] >= lo and a[1] <= hi and a[2] == e and not a[5])]
+                lst.append((lo, hi, e, sem, n, wr))
+
+    def emit(e, fn, R, W, dma=None):
+        R = [(b, 0, 512) if b[:2] == "ps" else (b, lo, hi) for (b, lo, hi) in R]
+        W = [(b, 0, 512) if b[:2] == "ps" else (b, lo, hi) for (b, lo, hi) in W]
+        waits(e, conflicts(e, R, W))
+        if dma is None:
+            cnt[e] += 1
+            sem, n, who = SEM[e], cnt[e], e
+            fn().then_inc(T.sem[sem], 1)
+        else:
+            sem, n = dma
+            who = "d" + sem
+            fn().then_inc(T.sem[sem], 16)
+        sn = dict(clk[e])
+        sn[sem] = n
+        snaps[(sem, n)] = sn
+        note(who, sem, n, R, W)
+
+    def ap(r):
+        return T[r[0]][:, r[1]:r[2]]
+
+    def ts(out, in0, s1, op0, s2=None, op1=None):
+        R = [in0] + [x for x in (s1, s2) if isinstance(x, tuple)]
+        a1 = ap(s1) if isinstance(s1, tuple) else s1
+        a2 = ap(s2) if isinstance(s2, tuple) else s2
+        if op1 is None:
+            emit("v", lambda: g.vector.tensor_scalar(out=ap(out), in0=ap(in0), scalar1=a1, scalar2=None, op0=op0), R, [out])
+        else:
+            emit("v", lambda: g.vector.tensor_scalar(out=ap(out), in0=ap(in0), scalar1=a1, scalar2=a2, op0=op0, op1=op1), R, [out])
+
+    def tt(out, in0, in1, op):
+        emit("v", lambda: g.vector.tensor_tensor(out=ap(out), in0=ap(in0), in1=ap(in1), op=op), [in0, in1], [out])
+
+    def cp(out, in_):
+        emit("v", lambda: g.vector.tensor_copy(out=ap(out), in_=ap(in_)), [in_], [out])
+
+    def fill(out, c):
+        emit("v", lambda: g.vector.memset(ap(out), c), [], [out])
+
+    def act(out, in_, func=F.Identity, bias=0.0, scale=1.0):
+        R = [in_]
+        sc = scale
+        if isinstance(scale, tuple):
+            R.append(scale)
+            sc = ap(scale)
+        emit("s", lambda: g.scalar.activation(out=ap(out), in_=ap(in_), func=func, bias=bias, scale=sc), R, [out])
+
+    def mm(out, lhsT, rhs, start, stop, a=0, step=1):
+        r = T[rhs[0]][:, rhs[1] + a:rhs[2]:step] if step > 1 else ap(rhs)
+        emit("t", lambda: g.tensor.matmul(out=ap(out), lhsT=ap(lhsT), rhs=r, start=start, stop=stop), [lhsT, rhs], [out])
+
+    def gat(e, out, win, offs, func=F.Identity, bias=0.0, scale=1.0):
+        if e == "v":
+            emit("v", lambda: g.vector.tensor_copy(out=ap(out), in_=ap(win).indirect(ap(offs))), [win, offs], [out])
+        else:
+            emit("s", lambda: g.scalar.activation(out=ap(out), in_=ap(win).indirect(ap(offs)), func=func, bias=bias, scale=scale), [win, offs], [out])
+
+    def iota(out, pattern, base, cm):
+        emit("g", lambda: g.iota(ap(out), pattern, base, cm, allow_small_or_imprecise_dtypes=True), [], [out])
+
+    def mat(i):
+        return ("mats", 128 * i, 128 * i + 128)
+    IB, I8, BO, NI8, B32, P512, N512, P8K, N8K, N4K, NIB, TRI = [mat(i) for i in range(12)]
+
+    def col16(b, i):
+        return (b, 128 * i, 128 * i + 128)
+
+    lsum = [0]
+    ready = []
+
+    def exchange(k):
+        w = WID[k]
+        snd = "snd%d" % k
+        for part in (p["far"], p["near"]):
+            if not part:
+                continue
+            i0 = order.index(part[0])
+            waits("g", conflicts("g", [(snd, i0 * w, (i0 + len(part)) * w)], []))
+            trs = []
+            for d in part:
+                i = order.index(d)
+                src = T[snd][:, i * w:(i + 1) * w]
+                if d in p["hop"]:
+                    to, dstap, sem = p["hop"][d], T["rb%d" % k][:, p["slot"][d] * w:(p["slot"][d] + 1) * w], T.sem["rl%d" % k]
+                else:
+                    to, dstap, sem = p["dst"][d], T["W%d" % k][:, (d - 1) * 128:(d - 1) * 128 + w], T.sem["arr%d" % k]
+                rid, pid = topo.addr(to, core)
+                trs.append(RemoteDMATransfer(dst_ids=[DstId(rid=rid, pnc=pid)], dma_engine_mask=bits(p["eng"][d]), remote_sem=sem, srcs=[src], dsts=[dstap]))
+                lsum[0] += len(p["eng"][d])
+            g.remote_dma_fused(trs, local_sem=T.sem.lsem)
+        tot = 0
+        n = len(T.cores)
+        for d in range(1, n):
+            q = plan(T.cores[(rank - d) % n], T, topo)
+            tot += len(topo.engines(q["hop"][d], core)) if d in q["hop"] else len(q["eng"][d])
+        for d in range(1, n):
+            note("d", "arr%d" % k, tot, [], [("W%d" % k, (d - 1) * 128, (d - 1) * 128 + w)])
+
+    def zero(reg):
+        act(reg, ("z", 0, reg[2] - reg[1]))
+
+    def zero_halves(k):
+        for d in range(7):
+            zero(("W%d" % k, d * 128 + 64, d * 128 + 128))
+
+    def shown(k, offs="shl", w4=4, srcreg=None):
+        win = srcreg or ("W%d" % k, NA, OWN + L + (CAP if k > 2 else 0))
+        e1 = nfar * w4
+        gat("v", ("snd%d" % k, 0, e1 * 16), win, (offs, 0, e1))
+        gat("s", ("snd%d" % k, e1 * 16, 7 * w4 * 16), win, (offs, e1, 7 * w4))
+        exchange(k)
+
+    ring = [0]
+    load = {"v": 0.0, "s": 0.0}
+
+    def landing(n):
+        r = ring[0] * NP * 16
+        ring[0] = (ring[0] + 1) % RING
+        return ("gr", r, r + n * 16)
+
+    def run_pass(k, groups, piece, chain, ev, es, delay=2, bg=(), v0=0.0):
+        active = [[0, b] for b in bg]
+        sums = []
+        npieces = sum(n // NP for _, n in groups)
+        load["v"], load["s"] = v0, 0.0
+
+        def step():
+            for a in list(active):
+                if a[0] > 0:
+                    a[0] -= 1
+                    continue
+                try:
+                    next(a[1])
+                except StopIteration:
+                    active.remove(a)
+
+        def add_up():
+            f = sums.pop(0)
+            f[0](*f[1:])
+        for gi, (c0, n) in enumerate(groups):
+            while c0 == L + CAP and not ready:
+                step()
+            gen = chain(gi, c0, n)
+            next(gen)
+            for x in range(0, n, NP):
+                load["v"] += ev / npieces
+                load["s"] += es / npieces
+                e = "v" if load["v"] <= load["s"] else "s"
+                load[e] += 16.0 * NP * 1.56 + (60 if e == "v" else 78)
+                gb = landing(NP)
+                offs = ("off", c0 + x, c0 + x + NP) if c0 < L + CAP else ("offo", x, x + NP)
+                gat(e, gb, ("W%d" % k, 0, WW), offs)
+                sums.append((piece, gi, c0, x, gb))
+                if len(sums) > LAG:
+                    add_up()
+                step()
+            active.append([delay + LAG, gen])
+        while active:
+            if sums:
+                add_up()
+            step()
+
+    emit("y", lambda: g.sync.dma_start(out=T.shi[:], in_=T.sh[:]), [], [("shi", 0, 28)], ("ld_sh", 16))
+    emit("y", lambda: g.sync.dma_start(out=T.W0[:, OWN:OWN + L], in_=T.v0[:]), [], [("W0", OWN, OWN + L)], ("ld_v", 16))
+    emit("s", lambda: g.scalar.dma_start(out=T.e32[:, 0:512], in_=T.e[:, 0:512]), [], [("e32", 0, 512)], ("ld_e0", 16))
+    emit("s", lambda: g.scalar.dma_start(out=T.e32[:, 512:1024], in_=T.e[:, 512:1024]), [], [("e32", 512, 1024)], ("ld_e1", 16))
+    emit("y", lambda: g.sync.dma_start(out=T.thi[:], in_=T.th[:]), [], [("thi", 0, 1)], ("ld_th", 16))
+    fill(("z", 0, 384), 0.0)
+    fill(("W0", NA, OWN), 0.0)
+    iota(("pc", 0, 1), [[0, 1]], 0, 1)
+    iota(("mi", 0, 128), [[1, 128]], 0, 0)
+    for i, d in enumerate(order):
+        ts(("shl", 4 * i, 4 * i + 4), ("shi", 4 * (d - 1), 4 * d), 8.0, A.add)
+    shown(0)
+    iota(("mg", 0, 128), [[1, 8], [0, 16]], 0, 0)
+    iota(("mm", 0, 128), [[0, 8], [1, 16]], 1, 0)
+    iota(("i16", 0, 16), [[1, 16]], 0, 0)
+    for h in (0, 512):
+        ts(("tf", h, h + 512), ("e32", h, h + 512), 1408.0, A.is_lt, 2312.0, A.mult)
+        tt(("tf", h, h + 512), ("e32", h, h + 512), ("tf", h, h + 512), A.add)
+        ts(("off", h, h + 512), ("tf", h, h + 512), -1408.0, A.add)
+        act(("ef", h, h + 512), ("tf", h, h + 512), bias=-2304.0)
+    zero(("W0", OWN + L, WW))
+    zero_halves(0)
+    for k in range(1, 7):
+        zero(("W%d" % k, NA, OWN))
+    fill(("ef", L, 1600), 0.0)
+    emit("v", lambda: g.vector.tensor_scalar(out=T.pc[:, 1:2], in0=T.pc[:, 0:1], scalar1=15, scalar2=None, op0=A.bitwise_and), [("pc", 0, 1)], [("pc", 1, 2)])
+    emit("v", lambda: g.vector.tensor_scalar(out=T.pc[:, 2:3], in0=T.pc[:, 0:1], scalar1=4, scalar2=None, op0=A.arith_shift_right), [("pc", 0, 1)], [("pc", 2, 3)])
+    cp(("pf", 0, 3), ("pc", 0, 3))
+    PCF, LANE, GRP = ("pf", 0, 1), ("pf", 1, 2), ("pf", 2, 3)
+    ts(IB, ("mi", 0, 128), PCF, A.is_equal)
+    ts(I8, IB, 0.125, A.mult)
+    fill(("cb1", 0, 256), -0.4375)
+    iota(("iotac", 0, 1024), [[1, 1024]], 0, 0)
+    iota(("padj", 0, 192), [[1, 192]], 1024, 0)
+    iota(("cposn", 0, 64), [[16, 64]], 192, 0)
+    iota(("hm", 0, NA), [[1, NA]], 64 - NA, 0)
+
+    def select_g(b, op, fill_):
+        R = [(b, 0, 2048)]
+        emit("g", lambda: g.affine_select(T[b][:], T[b][:], [[-1, 16], [0, 8], [1, 16]], op, fill_, 0, 0), R, R)
+        emit("g", lambda: g.affine_select(T[b][:], T[b][:], [[0, 16], [-16, 8], [0, 16]], A.is_ge, 0.0, 0, 1), R, R)
+        emit("g", lambda: g.affine_select(T[b][:], T[b][:], [[0, 16], [16, 8], [0, 16]], A.is_ge, 0.0, 15, -1), R, R)
+
+    fill(("pfx", 0, 2048), 1.0)
+    fill(("cola", 0, 2048), 1.0)
+    select_g("pfx", A.is_gt, -1.0)
+
+    def consts():
+        ts(BO, ("mg", 0, 128), GRP, A.is_equal)
+        for o, b, x in ((P512, IB, 512.0), (N512, IB, -512.0), (B32, BO, 32.0), (NI8, IB, -0.125), (P8K, IB, 8192.0), (N8K, IB, -8192.0), (N4K, IB, -4096.0), (NIB, IB, -1.0)):
+            act(o, b, scale=x)
+        cp(("thf", 0, 1), ("thi", 0, 1))
+        ts(("shm", 0, 28), ("shl", 0, 28), -8.0, A.add)
+        for i in range(7):
+            cp(("sh56", 8 * i, 8 * i + 4), ("shl", 4 * i, 4 * i + 4))
+        fill(("c192", 0, 1024), 192.0)
+        fill(("p0", 0, 1), 0.0)
+        fill(("p1", 0, 1), 0.0)
+        fill(("hb", L, L + CAP), 0.0)
+        ts(("cposn", 0, 64), ("cposn", 0, 64), LANE, A.add)
+        ts(("pf", 8, 9), LANE, 0.0, A.is_equal, 1.0e9, A.mult)
+        ts(("tmpc", 0, 128), ("mi", 0, 128), PCF, A.is_gt)
+        tt(("tmpc", 0, 128), ("tmpc", 0, 128), BO, A.mult)
+        tt(TRI, IB, ("tmpc", 0, 128), A.subtract)
+        ts(("lfc", 0, 16), ("i16", 0, 16), LANE, A.is_equal, 2.0 ** -10, A.mult)
+        ts(("lfc", 0, 16), ("lfc", 0, 16), 1.0, A.add)
+        for i in range(16):
+            ts(col16("lf", i), I8, ("lfc", i, i + 1), A.mult)
+        fill(("cb2", 0, 256), 15.5625)
+        fill(("cm1", 0, 256), -1.0)
+        fill(("cb3", 0, 256), 6528.0)
+        fill(("hm", NA, 2120), 0.0)
+        ts(("pf", 4, 5), LANE, 8.0, A.is_equal)
+        ts(("pf", 5, 6), LANE, 8.0, A.is_lt, -152.0, A.mult)
+        tt(("pf", 5, 6), ("pf", 5, 6), ("pf", 4, 5), A.subtract)
+        ts(("pf", 6, 7), ("pf", 4, 5), -64.0, A.mult)
+
+    def clip_piece(gi, c0, x, gb):
+        out = ("ps%d" % (gi % 4), x, x + NP)
+        mm(out, IB, ("cb1", 0, NP), True, False)
+        for i in range(16):
+            mm(out, I8, gb, False, i == 15, a=i, step=16)
+
+    def clip_chain(kin, kout, sums, hook=None):
+        def chain(gi, c0, n):
+            if hook:
+                hook(gi)
+            yield
+            tt(("ci", c0, c0 + n), ("ps%d" % (gi % 4), 0, n), ("W%d" % kin, OWN + c0, OWN + c0 + n), A.min)
+            cp(("W%d" % kout, OWN + c0, OWN + c0 + n), ("ci", c0, c0 + n))
+            if sums and c0 < L:
+                yield
+                b = "ps%d" % (4 + c0 // 512)
+                o = (b, c0 % 512, c0 % 512 + n)
+                r = ("W%d" % kout, OWN + c0, OWN + c0 + n)
+                if sums == 1:
+                    mm(o, BO, r, True, True)
+                else:
+                    mm(o, BO, r, True, False)
+                    mm(o, N8K, ("p0", c0 + 1, c0 + 1 + n), False, False)
+                    mm(o, P8K, ("p0", c0, c0 + n), False, True)
+                act(("hp", c0, c0 + n), r, scale=0.5, bias=128.25)
+                act(("hb", c0, c0 + n), ("hp", c0, c0 + n), bias=-128.0)
+                if sums == 1:
+                    act(("g2", c0, c0 + n), ("hp", c0, c0 + n), bias=-384.0)
+        return chain
+
+    G1024 = [(0, 256), (256, 256), (512, 256), (768, 128), (896, 128)]
+    G1216 = [(1024, 192)] + G1024
+
+    def select_states(P):
+        for h in (0, 512):
+            ts(("cand", h, h + 512), ("ps%d" % (4 + h // 512), 0, 512), ("thf", 0, 1), A.is_ge)
+            ini = 0.0 if h == 0 else T[P][:, 512:513]
+            rd = [("cand", h, h + 512), ("c192", h, h + 512)] + ([(P, 512, 513)] if h else [])
+            emit("v", lambda h=h, ini=ini: g.vector.tensor_tensor_scan(out=T[P][:, h + 1:h + 513], data0=T.cand[:, h:h + 512], data1=T.c192[:, h:h + 512], initial=ini, op0=A.add, op1=A.min),
+                 rd, [(P, h + 1, h + 513)])
+
+    def put_u(k, P, h, bk):
+        b = ("ps%d" % bk, 0, 512)
+        mm(b, IB, ("W%d" % k, OWN + h, OWN + h + 512), True, False)
+        mm(b, N512, (P, h + 1, h + 513), False, False)
+        mm(b, P512, (P, h, h + 512), False, True)
+        return b
+
+    def find_list(P, bk=(0, 1, 2)):
+        b0, b1, b2 = ("ps%d" % bk[0], 0, 64), ("ps%d" % bk[1], 0, 64), ("ps%d" % bk[2], 0, 12)
+        for a in range(16):
+            mm(b1, col16("cola", a), (P, 0, 1024), a == 0, a == 15, a=a, step=16)
+        for a in range(16):
+            mm(b0, col16("cola", a), (P, 1, 1025), a == 0, a == 15, a=a, step=16)
+        yield
+        cp(("lst", 0, 192), ("padj", 0, 192))
+        cp(("la", 0, 64), b1)
+        tt(("lb", 0, 64), b0, ("la", 0, 64), A.is_equal)
+        ts(("lc", 0, 64), b0, 0.0625, A.mult, -1.0, A.add)
+        ts(("lb", 0, 64), ("lb", 0, 64), 4096.0, A.mult)
+        tt(("lc", 0, 64), ("lc", 0, 64), ("lb", 0, 64), A.add)
+        tt(("lc", 0, 64), ("lc", 0, 64), ("cposn", 0, 64), A.min)
+        cp(("pos", 0, 64), ("lc", 0, 64))
+        yield
+        emit("v", lambda: g.vector.tensor_copy(out=T.lst[:, 0:1216].indirect(T.pos[:, 0:64]), in_=T.iotac[:, 0:1024]),
+             [("pos", 0, 64), ("iotac", 0, 1024)], [("lst", 0, 1216)])
+        cp(("l16", 0, 192), ("lst", 0, 192))
+        for a in range(16):
+            mm(b2, col16("cola", a), ("l16", 0, 192), a == 0, a == 15, a=a, step=16)
+        yield
+        ts(("slist", 0, 12), b2, 0.0625, A.mult)
+
+    SL = ("slist", 0, 12)
+
+    def cut(r, k, pb=3):
+        gat("v", ("old", 0, 192), ("ef", 0, 1216), SL)
+        ts(("offo", 0, 192), ("old", 0, 192), float(NA), A.add)
+        for x, e in ((0, "v"), (48, "s" if r == 0 else "v"), (96, "v"), (144, "s" if r == 0 else "v")):
+            gb = landing(48)
+            gat(e, gb, ("W%d" % k, 0, WW), ("offo", x, x + 48))
+            for i in range(16):
+                mm(("ps%d" % pb, x, x + 48), col16("pfx", i), gb, i == 0, i == 15, a=i, step=16)
+        yield
+        ts(("beh", 0, 192), ("ps%d" % pb, 0, 192), ("pf", 8, 9), A.is_ge)
+        hr = (L + CAP) + CAP * r
+        tt(("ef", hr, hr + 192), ("old", 0, 192), ("beh", 0, 192), A.mult)
+        emit("v", lambda: g.vector.tensor_tensor(out=T.ef[:, 0:1216].indirect(T.slist[:, 0:12]), in0=T.old[:, 0:192], in1=T.ef[:, hr:hr + 192], op=A.subtract),
+             [SL, ("old", 0, 192), ("ef", hr, hr + 192)], [("ef", 0, 1216)])
+
+    def ecol(c):
+        return c if c < L else c + CAP
+
+    def new_off(c0, n):
+        ts(("off", c0, c0 + n), ("ef", ecol(c0), ecol(c0) + n), float(NA), A.add)
+
+    run_pass(0, G1024, clip_piece, clip_chain(0, 1, 0), 2 * 1024, 0)
+    shown(1)
+    for k in range(1, 7):
+        if k in (1, 2, 6):
+            zero(("W%d" % k, OWN + L, WW))
+            zero_halves(k)
+        else:
+            zero(("W%d" % k, OWN + L + CAP, WW))
+    select_g("cola", A.is_equal, 0.0)
+    consts()
+    run_pass(1, G1024, clip_piece, clip_chain(1, 2, 1), 2 * 1024, 3 * 1024)
+    select_states("p0")
+    shown(2)
+    us = [put_u(2, "p0", h, 6 + h // 512) for h in (0, 512)]
+    for h in (0, 512):
+        tt(("W3", OWN + h, OWN + h + 512), us[h // 512], ("g2", h, h + 512), A.max)
+    gat("s", ("hs", 0, 448), ("hb", 0, L), ("shm", 0, 28))
+    gat("s", ("an", 0, 448), ("W3", NA, OWN + L), ("shl", 0, 28), func=F.Relu, scale=-1.0)
+    for i in range(7):
+        gat("v" if i < nfar else "s", ("snd3", 128 * i, 128 * i + 64), ("W3", NA, OWN + L), ("shl", 4 * i, 4 * i + 4))
+    for i in range(7):
+        tt(("snd3", 128 * i + 64, 128 * i + 128), ("hs", 64 * i, 64 * i + 64), ("an", 64 * i, 64 * i + 64), A.min)
+    exchange(3)
+    act(("xa", 0, L), ("W3", OWN, OWN + L), func=F.Abs, bias=128.0)
+    act(("xp", 0, L), ("xa", 0, L), func=F.Abs, bias=128.0, scale=-1.0)
+    for _ in find_list("p0"):
+        pass
+    gat("s", ("W3", OWN + L, OWN + L + CAP), ("hb", 0, L + CAP), SL)
+    for _ in cut(0, 2):
+        pass
+    new_off(L, CAP)
+    new_off(0, 256)
+    act(("xp", L, L + CAP), ("W3", OWN + L, OWN + L + CAP))
+
+    def half_list():
+        yield
+        yield
+        yield
+        emit("v", lambda: g.vector.tensor_scalar(out=T.hm[:, OWN:2120].indirect(T.slist[:, 0:12]), in0=T.padj[:, 0:192], scalar1=1.0, scalar2=8.0, op0=A.mult, op1=A.add),
+             [SL, ("padj", 0, 192)], [("hm", OWN, 2120)])
+        yield
+        gat("v", ("hg", 0, 448), ("hm", NA, 2120), ("shl", 0, 28))
+        for a in range(16):
+            mm(("ps7", 0, 28), col16("cola", a), ("hg", 0, 448), a == 0, a == 15, a=a, step=16)
+        yield
+        yield
+        yield
+        for i in range(7):
+            ts(("sh56", 8 * i + 4, 8 * i + 8), ("ps7", 4 * i, 4 * i + 4), 0.0625, A.mult)
+
+    def first_empty(c0, n):
+        ec = ecol(c0)
+        ts(("em", c0, c0 + n), ("ef", ec, ec + n), 0.0, A.is_equal, -4096.0, A.mult)
+        mm(("ps6", 0, n), TRI, ("em", c0, c0 + n), True, True)
+        act(("fe", c0, c0 + n), ("ps6", 0, n), func=F.Relu, scale=-1.0 / 4096)
+
+    GF = [(1024, 192), (0, 256), (256, 256), (512, 256), (768, 128), (896, 128)]
+
+    def fuse_piece(gi, c0, x, gb):
+        out = ("ps%d" % (gi % 3), x, x + NP)
+        for i in range(16):
+            mm(out, col16("lf", i), gb, i == 0, i == 15, a=i, step=16)
+
+    def fuse_chain(gi, c0, n):
+        rb, ub, tb, zb = "ps%d" % (gi % 3), "ps%d" % (3 + gi % 2), "ps5", "ps6"
+        c1 = c0 + n
+        ec = ecol(c0)
+        if 0 < gi < len(GF) - 1:
+            new_off(*GF[gi + 1])
+        first_empty(c0, n)
+        yield
+        ts(("k8", c0, c1), (rb, 0, n), MAGIC8, A.add, MAGIC8, A.subtract)
+        tt(("ff", c0, c1), (rb, 0, n), ("k8", c0, c1), A.is_lt)
+        mm((ub, 0, n), TRI, ("ff", c0, c1), True, False)
+        mm((ub, 0, n), BO, ("fe", c0, c1), False, False)
+        mm((ub, 0, n), IB, ("cm1", 0, n), False, True)
+        yield
+        act((ub, 0, n), (ub, 0, n), func=F.Relu)
+        for _ in range(Y1):
+            yield
+        tt(("fx", c0, c1), (ub, 0, n), ("ef", ec, ec + n), A.mult)
+        for a in range(16):
+            mm((tb, 0, n // 16), col16("cola", a), ("fx", c0, c1), a == 0, a == 15, a=a, step=16)
+        for _ in range(Y2):
+            yield
+        tl = ("tl", c0 // 16, c1 // 16)
+        ts(tl, (tb, 0, n // 16), float(NA), A.add)
+        gat("s", ("ab", c0, c1), ("W3", 0, WW), tl, func=F.Abs, bias=128.0)
+        for _ in range(Y3):
+            yield
+        mm((zb, 0, n), IB, ("cb2", 0, n), True, False)
+        mm((zb, 0, n), B32, ("ff", c0, c1), False, False)
+        mm((zb, 0, n), NI8, ("ab", c0, c1), False, True)
+        tt((zb, 0, n), (zb, 0, n), ("k8", c0, c1), A.add)
+        tt(("ci", c0, c1), (zb, 0, n), ("xp", c0, c1), A.min)
+        cp(("W4", OWN + c0, OWN + c1), ("ci", c0, c1))
+
+    run_pass(3, GF, fuse_piece, fuse_chain, 7 * 1216, 4.6 * 1216, bg=[half_list()])
+    shown(4, "sh56", 8)
+
+    def insert(c0, n):
+        c1, ec = c0 + n, ecol(c0)
+        emit("v", lambda: g.vector.tensor_tensor(out=T.tin[:, c0:c1], in0=T.hm[:, 0:2120].indirect(T.tl[:, c0 // 16:c1 // 16]), in1=T.fe[:, c0:c1], op=A.mult),
+             [("hm", 0, 2120), ("tl", c0 // 16, c1 // 16), ("fe", c0, c1)], [("tin", c0, c1)])
+        tt(("ef", ec, ec + n), ("ef", ec, ec + n), ("tin", c0, c1), A.add)
+        new_off(c0, n)
+
+    for c0, n in G1216[:3]:
+        insert(c0, n)
+
+    run_pass(4, G1216, clip_piece, clip_chain(4, 5, 2, lambda gi: insert(*G1216[gi + 2]) if 0 < gi < 4 else None), 2 * 1216 + 4.6 * 512, 2 * 1024)
+    select_states("p1")
+    for h in (0, 512):
+        b = ("ps%d" % (6 + h // 512), 0, 512)
+        mm(b, IB, ("p1", h + 1, h + 513), True, False)
+        mm(b, NIB, ("p1", h, h + 512), False, True)
+        act(("sfl", h, h + 512), b, scale=("pf", 6, 7))
+    shown(5, "sh56", 8)
+    shown(6, "shm", 4, srcreg=("sfl", 0, L))
+    fl = find_list("p1", (4, 5, 4))
+    next(fl)
+    ts(("cw", 0, L), ("p1", 1, L + 1), ("pf", 4, 5), A.mult, ("pf", 5, 6), A.add)
+    for h in (0, 512):
+        tt(("W6", OWN + h, OWN + h + 512), ("ps%d" % (6 + h // 512), 0, 512), ("cw", h, h + 512), A.mult)
+
+    def split_beside():
+        for _ in fl:
+            yield
+        yield
+        for _ in cut(1, 5, 5):
+            yield
+        ready.append(1)
+        yield
+        yield
+        gat("s", ("xp", L + CAP, V), ("hb", 0, L + CAP), SL)
+        for h in (0, 512):
+            b = put_u(5, "p1", h, 6)
+            tt(("xp", h, h + 512), b, ("hb", h, h + 512), A.max)
+            yield
+        emit("y", lambda: g.sync.dma_start(out=T.yv[:, 0:L], in_=T.xp[:, 0:L]), [("xp", 0, L)], [], ("stv", 16))
+        emit("y", lambda: g.sync.dma_start(out=T.yv[:, L:L + CAP], in_=T.W5[:, OWN + L:OWN + L + CAP]), [("W5", OWN + L, OWN + L + CAP)], [], ("stv", 32))
+        emit("y", lambda: g.sync.dma_start(out=T.yv[:, L + CAP:V], in_=T.xp[:, L + CAP:V]), [("xp", L + CAP, V)], [], ("stv", 48))
+
+    nst = [0]
+
+    def last_piece(gi, c0, x, gb):
+        out = ("ps%d" % (gi % 4), x, x + NP)
+        for i in range(16):
+            mm(out, col16("cola", i), gb, i == 0, i == 15, a=i, step=16)
+
+    def last_chain(gi, c0, n):
+        db, ub, xb = "ps%d" % (gi % 4), "ps%d" % (4 + 3 * (gi % 2)), "ps5"
+        c1 = c0 + n
+        ec = ecol(c0)
+        E = ("ef", ec, ec + n)
+        yield
+        while not ready:
+            yield
+        first_empty(c0, n)
+        act(("nm", c0, c1), E, func=F.Relu, scale=-1.0)
+        act(("zz", c0, c1), E, func=F.Sign, bias=-0.5)
+        act(("zz", c0, c1), ("zz", c0, c1), scale=-1156.0, bias=1148.0)
+        yield
+        tt(("ff", c0, c1), (db, 0, n), ("em", c0, c1), A.is_lt)
+        tt(("nc", c0, c1), (db, 0, n), ("nm", c0, c1), A.subtract)
+        mm((ub, 0, n), TRI, ("ff", c0, c1), True, True)
+        yield
+        act((ub, 0, n), (ub, 0, n), func=F.Relu)
+        yield
+        tt(("fx", c0, c1), (ub, 0, n), ("nc", c0, c1), A.mult)
+        mm((xb, 0, n), IB, ("cb3", 0, n), True, False)
+        mm((xb, 0, n), N4K, ("fe", c0, c1), False, False)
+        mm((xb, 0, n), BO, ("fx", c0, c1), False, True)
+        yield
+        tt(("et", c0, c1), E, ("zz", c0, c1), A.add)
+        tt(("yeb", c0, c1), (xb, 0, n), ("et", c0, c1), A.min)
+        nst[0] += 16
+        emit("y", lambda: g.sync.dma_start(out=T.ye[:, c0:c1], in_=T.yeb[:, c0:c1]), [("yeb", c0, c1)], [], ("sty", nst[0]))
+
+    GL = [(0, 256), (256, 256), (512, 256), (1024, 192), (1216, 192), (768, 128), (896, 128)]
+    run_pass(6, GL, last_piece, last_chain, 7 * 1408, 5 * 1408, bg=[split_beside()], v0=9000.0)
+
+    g.sync.wait_ge(T.sem.sty, nst[0])
+    g.sync.wait_ge(T.sem.stv, 48)
+    for e in ("v", "s", "t", "g"):
+        g.sync.wait_ge(T.sem[SEM[e]], cnt[e])
+    g.wait_ge(T.sem.lsem, lsum[0])

@@ -4,7 +4,8 @@ from concourse.mybir import dt, AluOpType as A, ActivationFunctionType as F
 NA, OWN, WW = 896, 904, 2312
 L, CAP, S, V = 1024, 192, 64, 1408
 NP = 64
-Y1, Y2, Y3 = 2, 2, 2
+YA, Y1, Y2, Y3 = 2, 2, 3, 2
+X1, X2, X3 = 1, 2, 2
 LAG = 2
 RING = 16
 WID = [64, 64, 64, 128, 128, 128, 64]
@@ -29,7 +30,7 @@ SCRATCH = {
     "hp": ("sbuf", [128, 1024], "bfloat16"), "hb": ("sbuf", [128, 1216], "bfloat16"), "g2": ("sbuf", [128, 1024], "bfloat16"),
     "xp": ("sbuf", [128, 1408], "bfloat16"), "hs": ("sbuf", [128, 448], "bfloat16"), "an": ("sbuf", [128, 448], "bfloat16"),
     "la": ("sbuf", [128, 64], "float32"), "lb": ("sbuf", [128, 64], "float32"), "lc": ("sbuf", [128, 64], "float32"),
-    "pos": ("sbuf", [128, 64], "uint16"), "lst": ("sbuf", [128, 1216], "float32"), "l16": ("sbuf", [128, 192], "float16"),
+    "pos": ("sbuf", [128, 64], "uint16"), "lst": ("sbuf", [128, 1408], "float32"), "l16": ("sbuf", [128, 192], "float16"),
     "slist": ("sbuf", [128, 12], "uint16"), "old": ("sbuf", [128, 192], "float32"), "offo": ("sbuf", [128, 192], "uint16"),
     "beh": ("sbuf", [128, 192], "float32"), "hm": ("sbuf", [128, 2120], "float32"), "hg": ("sbuf", [128, 448], "float16"),
     "em": ("sbuf", [128, 1408], "bfloat16"), "fe": ("sbuf", [128, 1408], "bfloat16"),
@@ -97,7 +98,7 @@ def relay_program(g, core, T, topo):
             if not mine:
                 return
             tot = 0
-            for k in range(7):
+            for k in [0, 1, 2, 3, 4, 6, 5]:
                 w = WID[k]
                 g.wait_ge(T.sem["rl%d" % k], sum(len(p["eng"][d]) for d in mine))
                 for d in mine:
@@ -271,12 +272,13 @@ def rank_program(g, core, T, topo):
         for d in range(7):
             zero(("W%d" % k, d * 128 + 64, d * 128 + 128))
 
-    def shown(k, offs="shl", w4=4, srcreg=None):
+    def shown(k, offs="shl", w4=4, srcreg=None, send=True, e0="v"):
         win = srcreg or ("W%d" % k, NA, OWN + L + (CAP if k > 2 else 0))
         e1 = nfar * w4
-        gat("v", ("snd%d" % k, 0, e1 * 16), win, (offs, 0, e1))
+        gat(e0, ("snd%d" % k, 0, e1 * 16), win, (offs, 0, e1))
         gat("s", ("snd%d" % k, e1 * 16, 7 * w4 * 16), win, (offs, e1, 7 * w4))
-        exchange(k)
+        if send:
+            exchange(k)
 
     ring = [0]
     load = {"v": 0.0, "s": 0.0}
@@ -362,17 +364,15 @@ def rank_program(g, core, T, topo):
     fill(("cb1", 0, 256), -0.4375)
     iota(("iotac", 0, 1024), [[1, 1024]], 0, 0)
     iota(("padj", 0, 192), [[1, 192]], 1024, 0)
-    iota(("cposn", 0, 64), [[16, 64]], 192, 0)
-    iota(("hm", 0, NA), [[1, NA]], 64 - NA, 0)
+    iota(("cposn", 0, 64), [[16, 64]], 193, 0)
 
     def select_g(b, op, fill_):
+        iota((b, 0, 2048), [[0, 2048]], 1, 0)
         R = [(b, 0, 2048)]
         emit("g", lambda: g.affine_select(T[b][:], T[b][:], [[-1, 16], [0, 8], [1, 16]], op, fill_, 0, 0), R, R)
         emit("g", lambda: g.affine_select(T[b][:], T[b][:], [[0, 16], [-16, 8], [0, 16]], A.is_ge, 0.0, 0, 1), R, R)
         emit("g", lambda: g.affine_select(T[b][:], T[b][:], [[0, 16], [16, 8], [0, 16]], A.is_ge, 0.0, 15, -1), R, R)
 
-    fill(("pfx", 0, 2048), 1.0)
-    fill(("cola", 0, 2048), 1.0)
     select_g("pfx", A.is_gt, -1.0)
 
     def consts():
@@ -383,7 +383,6 @@ def rank_program(g, core, T, topo):
         ts(("shm", 0, 28), ("shl", 0, 28), -8.0, A.add)
         for i in range(7):
             cp(("sh56", 8 * i, 8 * i + 4), ("shl", 4 * i, 4 * i + 4))
-        fill(("c192", 0, 1024), 192.0)
         fill(("p0", 0, 1), 0.0)
         fill(("p1", 0, 1), 0.0)
         fill(("hb", L, L + CAP), 0.0)
@@ -399,7 +398,6 @@ def rank_program(g, core, T, topo):
         fill(("cb2", 0, 256), 15.5625)
         fill(("cm1", 0, 256), -1.0)
         fill(("cb3", 0, 256), 6528.0)
-        fill(("hm", NA, 2120), 0.0)
         ts(("pf", 4, 5), LANE, 8.0, A.is_equal)
         ts(("pf", 5, 6), LANE, 8.0, A.is_lt, -152.0, A.mult)
         tt(("pf", 5, 6), ("pf", 5, 6), ("pf", 4, 5), A.subtract)
@@ -435,7 +433,7 @@ def rank_program(g, core, T, topo):
                     act(("g2", c0, c0 + n), ("hp", c0, c0 + n), bias=-384.0)
         return chain
 
-    G1024 = [(0, 256), (256, 256), (512, 256), (768, 128), (896, 128)]
+    G1024 = [(0, 256), (256, 256), (512, 256), (768, 192), (960, 64)]
     G1216 = [(1024, 192)] + G1024
 
     def select_states(P):
@@ -464,13 +462,12 @@ def rank_program(g, core, T, topo):
         cp(("la", 0, 64), b1)
         tt(("lb", 0, 64), b0, ("la", 0, 64), A.is_equal)
         ts(("lc", 0, 64), b0, 0.0625, A.mult, -1.0, A.add)
-        ts(("lb", 0, 64), ("lb", 0, 64), 4096.0, A.mult)
+        tt(("lb", 0, 64), ("lb", 0, 64), ("cposn", 0, 64), A.mult)
         tt(("lc", 0, 64), ("lc", 0, 64), ("lb", 0, 64), A.add)
-        tt(("lc", 0, 64), ("lc", 0, 64), ("cposn", 0, 64), A.min)
         cp(("pos", 0, 64), ("lc", 0, 64))
         yield
-        emit("v", lambda: g.vector.tensor_copy(out=T.lst[:, 0:1216].indirect(T.pos[:, 0:64]), in_=T.iotac[:, 0:1024]),
-             [("pos", 0, 64), ("iotac", 0, 1024)], [("lst", 0, 1216)])
+        emit("v", lambda: g.vector.tensor_copy(out=T.lst[:, 0:1408].indirect(T.pos[:, 0:64]), in_=T.iotac[:, 0:1024]),
+             [("pos", 0, 64), ("iotac", 0, 1024)], [("lst", 0, 1408)])
         cp(("l16", 0, 192), ("lst", 0, 192))
         for a in range(16):
             mm(b2, col16("cola", a), ("l16", 0, 192), a == 0, a == 15, a=a, step=16)
@@ -508,33 +505,41 @@ def rank_program(g, core, T, topo):
             zero_halves(k)
         else:
             zero(("W%d" % k, OWN + L + CAP, WW))
+    iota(("c192", 0, 1024), [[0, 1024]], 192, 0)
     select_g("cola", A.is_equal, 0.0)
     consts()
     run_pass(1, G1024, clip_piece, clip_chain(1, 2, 1), 2 * 1024, 3 * 1024)
     select_states("p0")
-    shown(2)
+    shown(2, e0="s")
     us = [put_u(2, "p0", h, 6 + h // 512) for h in (0, 512)]
     for h in (0, 512):
         tt(("W3", OWN + h, OWN + h + 512), us[h // 512], ("g2", h, h + 512), A.max)
     gat("s", ("hs", 0, 448), ("hb", 0, L), ("shm", 0, 28))
+    fl = find_list("p0")
+    next(fl)
     gat("s", ("an", 0, 448), ("W3", NA, OWN + L), ("shl", 0, 28), func=F.Relu, scale=-1.0)
     for i in range(7):
-        gat("v" if i < nfar else "s", ("snd3", 128 * i, 128 * i + 64), ("W3", NA, OWN + L), ("shl", 4 * i, 4 * i + 4))
+        gat("s", ("snd3", 128 * i, 128 * i + 64), ("W3", NA, OWN + L), ("shl", 4 * i, 4 * i + 4))
+    next(fl)
     for i in range(7):
+        if i == nfar:
+            next(fl)
         tt(("snd3", 128 * i + 64, 128 * i + 128), ("hs", 64 * i, 64 * i + 64), ("an", 64 * i, 64 * i + 64), A.min)
     exchange(3)
+    iota(("hm", 0, NA), [[1, NA]], 64 - NA, 0)
+    iota(("hm", NA, 2120), [[0, 2120 - NA]], 0, 0)
     act(("xa", 0, L), ("W3", OWN, OWN + L), func=F.Abs, bias=128.0)
     act(("xp", 0, L), ("xa", 0, L), func=F.Abs, bias=128.0, scale=-1.0)
-    for _ in find_list("p0"):
+    for _ in fl:
         pass
     gat("s", ("W3", OWN + L, OWN + L + CAP), ("hb", 0, L + CAP), SL)
     for _ in cut(0, 2):
         pass
     new_off(L, CAP)
-    new_off(0, 256)
     act(("xp", L, L + CAP), ("W3", OWN + L, OWN + L + CAP))
 
     def half_list():
+        new_off(0, 256)
         yield
         yield
         yield
@@ -556,7 +561,7 @@ def rank_program(g, core, T, topo):
         mm(("ps6", 0, n), TRI, ("em", c0, c0 + n), True, True)
         act(("fe", c0, c0 + n), ("ps6", 0, n), func=F.Relu, scale=-1.0 / 4096)
 
-    GF = [(1024, 192), (0, 256), (256, 256), (512, 256), (768, 128), (896, 128)]
+    GF = [(1024, 192), (0, 256), (256, 256), (512, 256), (768, 256)]
 
     def fuse_piece(gi, c0, x, gb):
         out = ("ps%d" % (gi % 3), x, x + NP)
@@ -564,11 +569,13 @@ def rank_program(g, core, T, topo):
             mm(out, col16("lf", i), gb, i == 0, i == 15, a=i, step=16)
 
     def fuse_chain(gi, c0, n):
-        rb, ub, tb, zb = "ps%d" % (gi % 3), "ps%d" % (3 + gi % 2), "ps5", "ps6"
+        rb, ub, tb, zb = "ps%d" % (gi % 3), "ps%d" % (3 + gi % 2), "ps%d" % (5 + 2 * (gi % 2)), "ps6"
         c1 = c0 + n
         ec = ecol(c0)
         if 0 < gi < len(GF) - 1:
             new_off(*GF[gi + 1])
+        if gi == 0:
+            yield
         first_empty(c0, n)
         yield
         ts(("k8", c0, c1), (rb, 0, n), MAGIC8, A.add, MAGIC8, A.subtract)
@@ -576,7 +583,8 @@ def rank_program(g, core, T, topo):
         mm((ub, 0, n), TRI, ("ff", c0, c1), True, False)
         mm((ub, 0, n), BO, ("fe", c0, c1), False, False)
         mm((ub, 0, n), IB, ("cm1", 0, n), False, True)
-        yield
+        for _ in range(YA):
+            yield
         act((ub, 0, n), (ub, 0, n), func=F.Relu)
         for _ in range(Y1):
             yield
@@ -597,7 +605,7 @@ def rank_program(g, core, T, topo):
         tt(("ci", c0, c1), (zb, 0, n), ("xp", c0, c1), A.min)
         cp(("W4", OWN + c0, OWN + c1), ("ci", c0, c1))
 
-    run_pass(3, GF, fuse_piece, fuse_chain, 7 * 1216, 4.6 * 1216, bg=[half_list()])
+    run_pass(3, GF, fuse_piece, fuse_chain, 10 * 1216, 5 * 1216, 0, bg=[half_list()])
     shown(4, "sh56", 8)
 
     def insert(c0, n):
@@ -610,15 +618,16 @@ def rank_program(g, core, T, topo):
     for c0, n in G1216[:3]:
         insert(c0, n)
 
-    run_pass(4, G1216, clip_piece, clip_chain(4, 5, 2, lambda gi: insert(*G1216[gi + 2]) if 0 < gi < 4 else None), 2 * 1216 + 4.6 * 512, 2 * 1024)
+    run_pass(4, G1216, clip_piece, clip_chain(4, 5, 2, lambda gi: insert(*G1216[gi + 2]) if 0 < gi < 4 else None), 6 * 1216, 1.7 * 1216, 2)
     select_states("p1")
     for h in (0, 512):
         b = ("ps%d" % (6 + h // 512), 0, 512)
         mm(b, IB, ("p1", h + 1, h + 513), True, False)
         mm(b, NIB, ("p1", h, h + 512), False, True)
         act(("sfl", h, h + 512), b, scale=("pf", 6, 7))
-    shown(5, "sh56", 8)
+    shown(5, "sh56", 8, send=False)
     shown(6, "shm", 4, srcreg=("sfl", 0, L))
+    exchange(5)
     fl = find_list("p1", (4, 5, 4))
     next(fl)
     ts(("cw", 0, L), ("p1", 1, L + 1), ("pf", 4, 5), A.mult, ("pf", 5, 6), A.add)
@@ -661,26 +670,29 @@ def rank_program(g, core, T, topo):
         first_empty(c0, n)
         act(("nm", c0, c1), E, func=F.Relu, scale=-1.0)
         act(("zz", c0, c1), E, func=F.Sign, bias=-0.5)
-        act(("zz", c0, c1), ("zz", c0, c1), scale=-1156.0, bias=1148.0)
         yield
         tt(("ff", c0, c1), (db, 0, n), ("em", c0, c1), A.is_lt)
         tt(("nc", c0, c1), (db, 0, n), ("nm", c0, c1), A.subtract)
         mm((ub, 0, n), TRI, ("ff", c0, c1), True, True)
-        yield
+        for _ in range(X1):
+            yield
         act((ub, 0, n), (ub, 0, n), func=F.Relu)
-        yield
+        for _ in range(X2):
+            yield
         tt(("fx", c0, c1), (ub, 0, n), ("nc", c0, c1), A.mult)
         mm((xb, 0, n), IB, ("cb3", 0, n), True, False)
         mm((xb, 0, n), N4K, ("fe", c0, c1), False, False)
         mm((xb, 0, n), BO, ("fx", c0, c1), False, True)
-        yield
-        tt(("et", c0, c1), E, ("zz", c0, c1), A.add)
+        act((xb, 256, 256 + n), ("zz", c0, c1), scale=-1156.0, bias=1148.0)
+        for _ in range(X3):
+            yield
+        tt(("et", c0, c1), E, (xb, 256, 256 + n), A.add)
         tt(("yeb", c0, c1), (xb, 0, n), ("et", c0, c1), A.min)
         nst[0] += 16
         emit("y", lambda: g.sync.dma_start(out=T.ye[:, c0:c1], in_=T.yeb[:, c0:c1]), [("yeb", c0, c1)], [], ("sty", nst[0]))
 
-    GL = [(0, 256), (256, 256), (512, 256), (1024, 192), (1216, 192), (768, 128), (896, 128)]
-    run_pass(6, GL, last_piece, last_chain, 7 * 1408, 5 * 1408, bg=[split_beside()], v0=9000.0)
+    GL = [(0, 256), (256, 256), (512, 256), (1024, 192), (768, 128), (1216, 192), (896, 128)]
+    run_pass(6, GL, last_piece, last_chain, 7 * 1408, 5 * 1408, 2, bg=[split_beside()], v0=6000.0)
 
     g.sync.wait_ge(T.sem.sty, nst[0])
     g.sync.wait_ge(T.sem.stv, 48)

from concourse.bass import DstId, RemoteDMATransfer
from concourse.mybir import dt, AluOpType as A, ActivationFunctionType as F

NA, OWN, WW = 896, 904, 2312
L, CAP, S, V = 1024, 192, 64, 1408
NP = 64
YA, Y1, Y2, Y3 = 2, 2, 3, 2
X1, X2, X3 = 1, 2, 2
LAG = 2
RING = 16
WID = [64, 64, 64, 128, 128, 128, 64]
MAGIC8 = 1572864.0

SCRATCH = {
    "shi": ("sbuf", [128, 28], "int32"), "thi": ("sbuf", [128, 1], "int32"), "e32": ("sbuf", [128, 1024], "int32"),
    "shl": ("sbuf", [128, 28], "uint16"), "shm": ("sbuf", [128, 28], "uint16"), "sh56": ("sbuf", [128, 56], "uint16"),
    "z": ("sbuf", [128, 384], "bfloat16"), "xa": ("sbuf", [128, 1024], "float32"),
    "off": ("sbuf", [128, 1408], "uint16"), "ef": ("sbuf", [128, 1600], "float32"), "tf": ("sbuf", [128, 1024], "float32"),
    "gr": ("sbuf", [128, RING * NP * 16], "bfloat16"), "ci": ("sbuf", [128, 1216], "int32"),
    "thf": ("sbuf", [128, 1], "float32"),
    "pc": ("sbuf", [128, 4], "int32"), "pf": ("sbuf", [128, 16], "float32"),
    "mi": ("sbuf", [128, 128], "float32"), "mg": ("sbuf", [128, 128], "float32"), "mm": ("sbuf", [128, 128], "float32"),
    "i16": ("sbuf", [128, 16], "float32"), "lfc": ("sbuf", [128, 16], "float32"), "tmpc": ("sbuf", [128, 128], "float32"),
    "mats": ("sbuf", [128, 16 * 128], "bfloat16"), "cola": ("sbuf", [128, 2048], "bfloat16"),
    "pfx": ("sbuf", [128, 2048], "bfloat16"), "lf": ("sbuf", [128, 2048], "float16"),
    "cposn": ("sbuf", [128, 64], "float32"), "iotac": ("sbuf", [128, 1024], "float32"), "padj": ("sbuf", [128, 192], "float32"),
    "c192": ("sbuf", [128, 1024], "bfloat16"), "cb1": ("sbuf", [128, 256], "bfloat16"), "cb2": ("sbuf", [128, 256], "bfloat16"),
    "cb3": ("sbuf", [128, 256], "bfloat16"), "cm1": ("sbuf", [128, 256], "bfloat16"),
    "cand": ("sbuf", [128, 1024], "bfloat16"), "p0": ("sbuf", [128, 1040], "bfloat16"), "p1": ("sbuf", [128, 1040], "bfloat16"),
    "hp": ("sbuf", [128, 1024], "bfloat16"), "hb": ("sbuf", [128, 1216], "bfloat16"), "g2": ("sbuf", [128, 1024], "bfloat16"),
    "xp": ("sbuf", [128, 1408], "bfloat16"), "hs": ("sbuf", [128, 448], "bfloat16"), "an": ("sbuf", [128, 448], "bfloat16"),
    "la": ("sbuf", [128, 64], "float32"), "lb": ("sbuf", [128, 64], "float32"), "lc": ("sbuf", [128, 64], "float32"),
    "pos": ("sbuf", [128, 64], "uint16"), "lst": ("sbuf", [128, 1408], "float32"), "l16": ("sbuf", [128, 192], "float16"),
    "slist": ("sbuf", [128, 12], "uint16"), "old": ("sbuf", [128, 192], "float32"), "offo": ("sbuf", [128, 192], "uint16"),
    "beh": ("sbuf", [128, 192], "float32"), "hm": ("sbuf", [128, 2120], "float32"), "hg": ("sbuf", [128, 448], "float16"),
    "em": ("sbuf", [128, 1408], "bfloat16"), "fe": ("sbuf", [128, 1408], "bfloat16"),
    "k8": ("sbuf", [128, 1216], "float32"), "ff": ("sbuf", [128, 1408], "bfloat16"), "fx": ("sbuf", [128, 1408], "float16"),
    "tl": ("sbuf", [128, 76], "uint16"), "ab": ("sbuf", [128, 1216], "bfloat16"), "tin": ("sbuf", [128, 1216], "float32"),
    "nm": ("sbuf", [128, 1408], "float32"), "zz": ("sbuf", [128, 1408], "float32"), "et": ("sbuf", [128, 1408], "float32"),
    "nc": ("sbuf", [128, 1408], "float16"), "yeb": ("sbuf", [128, 1408], "float32"),
    "cw": ("sbuf", [128, 1024], "bfloat16"), "sfl": ("sbuf", [128, 1024], "bfloat16"),
}
for _k in range(7):
    SCRATCH["W%d" % _k] = ("sbuf", [128, WW], "bfloat16")
    SCRATCH["snd%d" % _k] = ("sbuf", [128, 7 * WID[_k]], "bfloat16")
    SCRATCH["rb%d" % _k] = ("sbuf", [128, 4 * WID[_k]], "bfloat16")
for _k in range(8):
    SCRATCH["ps%d" % _k] = ("psum", [128, 512], "float32")
LOADS = ["ld_sh", "ld_th", "ld_v", "ld_e0", "ld_e1"]
SEMAPHORES = (["qv", "qs", "qt", "qg", "lsem", "sty", "stv"] + LOADS + ["arr%d" % k for k in range(7)] + ["rl%d" % k for k in range(7)])


def split_engines(engs, n):
    c = 1
    while c * 2 * n <= len(engs):
        c *= 2
    cnt = [c] * n
    left = len(engs) - c * n
    for i in range(n):
        if left >= cnt[i]:
            left -= cnt[i]
            cnt[i] *= 2
    out, at = [], 0
    for x in cnt:
        out.append(engs[at:at + x])
        at += x
    return out


def bits(engs):
    m = 0
    for x in engs:
        m |= 1 << x
    return m


def plan(core, T, topo):
    n = len(T.cores)
    me = T.rank_of(core)
    dst = {d: T.cores[(me + d) % n] for d in range(1, n)}
    far = [d for d in range(1, n) if not topo.may_write(core, dst[d])]
    near = [d for d in range(1, n) if topo.may_write(core, dst[d])]
    rel = [c for c in topo.cores_of(core) if c != core and all(topo.may_write(c, dst[d]) for d in far)]
    rel = sorted(rel, key=lambda c: (topo.die(c) != topo.die(core), c))
    hop = {d: rel[i % len(rel)] for i, d in enumerate(far)}
    slot = {d: i // len(rel) for i, d in enumerate(far)}
    e1 = split_engines(topo.engines(core, rel[0]), len(far))
    e2 = split_engines(topo.engines(core, dst[near[0]]), len(near))
    return {"dst": dst, "far": far, "near": near, "hop": hop, "slot": slot,
            "eng": {**{d: e1[i] for i, d in enumerate(far)}, **{d: e2[i] for i, d in enumerate(near)}}}


def relay_program(g, core, T, topo):
    for src in T.cores:
        if src in topo.cores_of(core):
            p = plan(src, T, topo)
            mine = [d for d in p["far"] if p["hop"][d] == core]
            if not mine:
                return
            tot = 0
            for k in [0, 1, 2, 3, 4, 6, 5]:
                w = WID[k]
                g.wait_ge(T.sem["rl%d" % k], sum(len(p["eng"][d]) for d in mine))
                for d in mine:
                    rid, pid = topo.addr(p["dst"][d], core)
                    en = topo.engines(core, p["dst"][d])
                    g.remote_dma(out_ap=T["W%d" % k][:, (d - 1) * 128:(d - 1) * 128 + w],
                                 in_ap=T["rb%d" % k][:, p["slot"][d] * w:(p["slot"][d] + 1) * w],
                                 remote_sem=T.sem["arr%d" % k], local_sem=T.sem.lsem, pid=pid, routing_id=rid, dma_engine_mask=bits(en))
                    tot += len(en)
            g.wait_ge(T.sem.lsem, tot)


def rank_program(g, core, T, topo):
    rank = T.rank_of(core)
    if rank is None:
        relay_program(g, core, T, topo)
        return
    p = plan(core, T, topo)
    order = p["far"] + p["near"]
    nfar = len(p["far"])
    Q = {"v": g.vector, "s": g.scalar, "t": g.tensor, "g": g, "y": g.sync}
    SEM = {"v": "qv", "s": "qs", "t": "qt", "g": "qg"}
    cnt = {"v": 0, "s": 0, "t": 0, "g": 0}
    clk = {e: {} for e in Q}
    snaps = {}
    acc = {}

    def conflicts(e, R, W):
        need = {}
        for wr, regs in ((False, R), (True, W)):
            for (b, lo, hi) in regs:
                ps = b[:2] == "ps"
                for (alo, ahi, ae, asem, an, aw) in acc.get(b, ()):
                    if ahi <= lo or hi <= alo:
                        continue
                    if ps and ae == e == "t":
                        continue
                    if not (wr or aw) and (ae == e or not ps):
                        continue
                    if clk[e].get(asem, 0) < an:
                        need[asem] = max(need.get(asem, 0), an)
        return need

    def waits(e, need):
        todo = sorted(need.items())
        drop = set()
        for (s, n) in todo:
            for (s2, n2) in todo:
                if s2 != s and s2 not in drop and snaps.get((s2, n2), {}).get(s, 0) >= n:
                    drop.add(s)
        for (s, n) in todo:
            if s in drop:
                continue
            Q[e].wait_ge(T.sem[s], n)
            clk[e][s] = max(clk[e].get(s, 0), n)
            for k2, v2 in snaps.get((s, n), {}).items():
                if clk[e].get(k2, 0) < v2:
                    clk[e][k2] = v2

    def note(e, sem, n, R, W):
        for wr, regs in ((False, R), (True, W)):
            for (b, lo, hi) in regs:
                lst = acc.setdefault(b, [])
                if wr:
                    lst[:] = [a for a in lst if not (a[0] >= lo and a[1] <= hi)]
                else:
                    lst[:] = [a for a in lst if not (a[0] >= lo and a[1] <= hi and a[2] == e and not a[5])]
                lst.append((lo, hi, e, sem, n, wr))

    def emit(e, fn, R, W, dma=None):
        R = [(b, 0, 512) if b[:2] == "ps" else (b, lo, hi) for (b, lo, hi) in R]
        W = [(b, 0, 512) if b[:2] == "ps" else (b, lo, hi) for (b, lo, hi) in W]
        waits(e, conflicts(e, R, W))
        if dma is None:
            cnt[e] += 1
            sem, n, who = SEM[e], cnt[e], e
            fn().then_inc(T.sem[sem], 1)
        else:
            sem, n = dma
            who = "d" + sem
            fn().then_inc(T.sem[sem], 16)
        sn = dict(clk[e])
        sn[sem] = n
        snaps[(sem, n)] = sn
        note(who, sem, n, R, W)

    def ap(r):
        return T[r[0]][:, r[1]:r[2]]

    def ts(out, in0, s1, op0, s2=None, op1=None):
        R = [in0] + [x for x in (s1, s2) if isinstance(x, tuple)]
        a1 = ap(s1) if isinstance(s1, tuple) else s1
        a2 = ap(s2) if isinstance(s2, tuple) else s2
        if op1 is None:
            emit("v", lambda: g.vector.tensor_scalar(out=ap(out), in0=ap(in0), scalar1=a1, scalar2=None, op0=op0), R, [out])
        else:
            emit("v", lambda: g.vector.tensor_scalar(out=ap(out), in0=ap(in0), scalar1=a1, scalar2=a2, op0=op0, op1=op1), R, [out])

    def tt(out, in0, in1, op):
        emit("v", lambda: g.vector.tensor_tensor(out=ap(out), in0=ap(in0), in1=ap(in1), op=op), [in0, in1], [out])

    def cp(out, in_):
        emit("v", lambda: g.vector.tensor_copy(out=ap(out), in_=ap(in_)), [in_], [out])

    def fill(out, c):
        emit("v", lambda: g.vector.memset(ap(out), c), [], [out])

    def act(out, in_, func=F.Identity, bias=0.0, scale=1.0):
        R = [in_]
        sc = scale
        if isinstance(scale, tuple):
            R.append(scale)
            sc = ap(scale)
        emit("s", lambda: g.scalar.activation(out=ap(out), in_=ap(in_), func=func, bias=bias, scale=sc), R, [out])

    def mm(out, lhsT, rhs, start, stop, a=0, step=1):
        r = T[rhs[0]][:, rhs[1] + a:rhs[2]:step] if step > 1 else ap(rhs)
        emit("t", lambda: g.tensor.matmul(out=ap(out), lhsT=ap(lhsT), rhs=r, start=start, stop=stop), [lhsT, rhs], [out])

    def gat(e, out, win, offs, func=F.Identity, bias=0.0, scale=1.0):
        if e == "v":
            emit("v", lambda: g.vector.tensor_copy(out=ap(out), in_=ap(win).indirect(ap(offs))), [win, offs], [out])
        else:
            emit("s", lambda: g.scalar.activation(out=ap(out), in_=ap(win).indirect(ap(offs)), func=func, bias=bias, scale=scale), [win, offs], [out])

    def iota(out, pattern, base, cm):
        emit("g", lambda: g.iota(ap(out), pattern, base, cm, allow_small_or_imprecise_dtypes=True), [], [out])

    def mat(i):
        return ("mats", 128 * i, 128 * i + 128)
    IB, I8, BO, NI8, B32, P512, N512, P8K, N8K, N4K, NIB, TRI = [mat(i) for i in range(12)]

    def col16(b, i):
        return (b, 128 * i, 128 * i + 128)

    lsum = [0]
    ready = []

    def exchange(k):
        w = WID[k]
        snd = "snd%d" % k
        for part in (p["far"], p["near"]):
            if not part:
                continue
            i0 = order.index(part[0])
            waits("g", conflicts("g", [(snd, i0 * w, (i0 + len(part)) * w)], []))
            trs = []
            for d in part:
                i = order.index(d)
                src = T[snd][:, i * w:(i + 1) * w]
                if d in p["hop"]:
                    to, dstap, sem = p["hop"][d], T["rb%d" % k][:, p["slot"][d] * w:(p["slot"][d] + 1) * w], T.sem["rl%d" % k]
                else:
                    to, dstap, sem = p["dst"][d], T["W%d" % k][:, (d - 1) * 128:(d - 1) * 128 + w], T.sem["arr%d" % k]
                rid, pid = topo.addr(to, core)
                trs.append(RemoteDMATransfer(dst_ids=[DstId(rid=rid, pnc=pid)], dma_engine_mask=bits(p["eng"][d]), remote_sem=sem, srcs=[src], dsts=[dstap]))
                lsum[0] += len(p["eng"][d])
            g.remote_dma_fused(trs, local_sem=T.sem.lsem)
        tot = 0
        n = len(T.cores)
        for d in range(1, n):
            q = plan(T.cores[(rank - d) % n], T, topo)
            tot += len(topo.engines(q["hop"][d], core)) if d in q["hop"] else len(q["eng"][d])
        for d in range(1, n):
            note("d", "arr%d" % k, tot, [], [("W%d" % k, (d - 1) * 128, (d - 1) * 128 + w)])

    def zero(reg):
        act(reg, ("z", 0, reg[2] - reg[1]))

    def zero_halves(k):
        for d in range(7):
            zero(("W%d" % k, d * 128 + 64, d * 128 + 128))

    def shown(k, offs="shl", w4=4, srcreg=None, send=True, e0="v"):
        win = srcreg or ("W%d" % k, NA, OWN + L + (CAP if k > 2 else 0))
        e1 = nfar * w4
        gat(e0, ("snd%d" % k, 0, e1 * 16), win, (offs, 0, e1))
        gat("s", ("snd%d" % k, e1 * 16, 7 * w4 * 16), win, (offs, e1, 7 * w4))
        if send:
            exchange(k)

    ring = [0]
    load = {"v": 0.0, "s": 0.0}

    def landing(n):
        r = ring[0] * NP * 16
        ring[0] = (ring[0] + 1) % RING
        return ("gr", r, r + n * 16)

    def run_pass(k, groups, piece, chain, ev, es, delay=2, bg=(), v0=0.0):
        active = [[0, b] for b in bg]
        sums = []
        npieces = sum(n // NP for _, n in groups)
        load["v"], load["s"] = v0, 0.0

        def step():
            for a in list(active):
                if a[0] > 0:
                    a[0] -= 1
                    continue
                try:
                    next(a[1])
                except StopIteration:
                    active.remove(a)

        def add_up():
            f = sums.pop(0)
            f[0](*f[1:])
        for gi, (c0, n) in enumerate(groups):
            while c0 == L + CAP and not ready:
                step()
            gen = chain(gi, c0, n)
            next(gen)
            for x in range(0, n, NP):
                load["v"] += ev / npieces
                load["s"] += es / npieces
                e = "v" if load["v"] <= load["s"] else "s"
                load[e] += 16.0 * NP * 1.56 + (60 if e == "v" else 78)
                gb = landing(NP)
                offs = ("off", c0 + x, c0 + x + NP) if c0 < L + CAP else ("offo", x, x + NP)
                gat(e, gb, ("W%d" % k, 0, WW), offs)
                sums.append((piece, gi, c0, x, gb))
                if len(sums) > LAG:
                    add_up()
                step()
            active.append([delay + LAG, gen])
        while active:
            if sums:
                add_up()
            step()

    emit("y", lambda: g.sync.dma_start(out=T.shi[:], in_=T.sh[:]), [], [("shi", 0, 28)], ("ld_sh", 16))
    emit("y", lambda: g.sync.dma_start(out=T.W0[:, OWN:OWN + L], in_=T.v0[:]), [], [("W0", OWN, OWN + L)], ("ld_v", 16))
    emit("s", lambda: g.scalar.dma_start(out=T.e32[:, 0:512], in_=T.e[:, 0:512]), [], [("e32", 0, 512)], ("ld_e0", 16))
    emit("s", lambda: g.scalar.dma_start(out=T.e32[:, 512:1024], in_=T.e[:, 512:1024]), [], [("e32", 512, 1024)], ("ld_e1", 16))
    emit("y", lambda: g.sync.dma_start(out=T.thi[:], in_=T.th[:]), [], [("thi", 0, 1)], ("ld_th", 16))
    fill(("z", 0, 384), 0.0)
    fill(("W0", NA, OWN), 0.0)
    iota(("pc", 0, 1), [[0, 1]], 0, 1)
    iota(("mi", 0, 128), [[1, 128]], 0, 0)
    for i, d in enumerate(order):
        ts(("shl", 4 * i, 4 * i + 4), ("shi", 4 * (d - 1), 4 * d), 8.0, A.add)
    shown(0)
    iota(("mg", 0, 128), [[1, 8], [0, 16]], 0, 0)
    iota(("mm", 0, 128), [[0, 8], [1, 16]], 1, 0)
    iota(("i16", 0, 16), [[1, 16]], 0, 0)
    for h in (0, 512):
        ts(("tf", h, h + 512), ("e32", h, h + 512), 1408.0, A.is_lt, 2312.0, A.mult)
        tt(("tf", h, h + 512), ("e32", h, h + 512), ("tf", h, h + 512), A.add)
        ts(("off", h, h + 512), ("tf", h, h + 512), -1408.0, A.add)
        act(("ef", h, h + 512), ("tf", h, h + 512), bias=-2304.0)
    zero(("W0", OWN + L, WW))
    zero_halves(0)
    for k in range(1, 7):
        zero(("W%d" % k, NA, OWN))
    fill(("ef", L, 1600), 0.0)
    emit("v", lambda: g.vector.tensor_scalar(out=T.pc[:, 1:2], in0=T.pc[:, 0:1], scalar1=15, scalar2=None, op0=A.bitwise_and), [("pc", 0, 1)], [("pc", 1, 2)])
    emit("v", lambda: g.vector.tensor_scalar(out=T.pc[:, 2:3], in0=T.pc[:, 0:1], scalar1=4, scalar2=None, op0=A.arith_shift_right), [("pc", 0, 1)], [("pc", 2, 3)])
    cp(("pf", 0, 3), ("pc", 0, 3))
    PCF, LANE, GRP = ("pf", 0, 1), ("pf", 1, 2), ("pf", 2, 3)
    ts(IB, ("mi", 0, 128), PCF, A.is_equal)
    ts(I8, IB, 0.125, A.mult)
    fill(("cb1", 0, 256), -0.4375)
    iota(("iotac", 0, 1024), [[1, 1024]], 0, 0)
    iota(("padj", 0, 192), [[1, 192]], 1024, 0)
    iota(("cposn", 0, 64), [[16, 64]], 193, 0)

    def select_g(b, op, fill_):
        iota((b, 0, 2048), [[0, 2048]], 1, 0)
        R = [(b, 0, 2048)]
        emit("g", lambda: g.affine_select(T[b][:], T[b][:], [[-1, 16], [0, 8], [1, 16]], op, fill_, 0, 0), R, R)
        emit("g", lambda: g.affine_select(T[b][:], T[b][:], [[0, 16], [-16, 8], [0, 16]], A.is_ge, 0.0, 0, 1), R, R)
        emit("g", lambda: g.affine_select(T[b][:], T[b][:], [[0, 16], [16, 8], [0, 16]], A.is_ge, 0.0, 15, -1), R, R)

    select_g("pfx", A.is_gt, -1.0)

    def consts():
        ts(BO, ("mg", 0, 128), GRP, A.is_equal)
        for o, b, x in ((P512, IB, 512.0), (N512, IB, -512.0), (B32, BO, 32.0), (NI8, IB, -0.125), (P8K, IB, 8192.0), (N8K, IB, -8192.0), (N4K, IB, -4096.0), (NIB, IB, -1.0)):
            act(o, b, scale=x)
        cp(("thf", 0, 1), ("thi", 0, 1))
        ts(("shm", 0, 28), ("shl", 0, 28), -8.0, A.add)
        for i in range(7):
            cp(("sh56", 8 * i, 8 * i + 4), ("shl", 4 * i, 4 * i + 4))
        fill(("p0", 0, 1), 0.0)
        fill(("p1", 0, 1), 0.0)
        fill(("hb", L, L + CAP), 0.0)
        ts(("cposn", 0, 64), ("cposn", 0, 64), LANE, A.add)
        ts(("pf", 8, 9), LANE, 0.0, A.is_equal, 1.0e9, A.mult)
        ts(("tmpc", 0, 128), ("mi", 0, 128), PCF, A.is_gt)
        tt(("tmpc", 0, 128), ("tmpc", 0, 128), BO, A.mult)
        tt(TRI, IB, ("tmpc", 0, 128), A.subtract)
        ts(("lfc", 0, 16), ("i16", 0, 16), LANE, A.is_equal, 2.0 ** -10, A.mult)
        ts(("lfc", 0, 16), ("lfc", 0, 16), 1.0, A.add)
        for i in range(16):
            ts(col16("lf", i), I8, ("lfc", i, i + 1), A.mult)
        fill(("cb2", 0, 256), 15.5625)
        fill(("cm1", 0, 256), -1.0)
        fill(("cb3", 0, 256), 6528.0)
        ts(("pf", 4, 5), LANE, 8.0, A.is_equal)
        ts(("pf", 5, 6), LANE, 8.0, A.is_lt, -152.0, A.mult)
        tt(("pf", 5, 6), ("pf", 5, 6), ("pf", 4, 5), A.subtract)
        ts(("pf", 6, 7), ("pf", 4, 5), -64.0, A.mult)

    def clip_piece(gi, c0, x, gb):
        out = ("ps%d" % (gi % 4), x, x + NP)
        mm(out, IB, ("cb1", 0, NP), True, False)
        for i in range(16):
            mm(out, I8, gb, False, i == 15, a=i, step=16)

    def clip_chain(kin, kout, sums, hook=None):
        def chain(gi, c0, n):
            if hook:
                hook(gi)
            yield
            tt(("ci", c0, c0 + n), ("ps%d" % (gi % 4), 0, n), ("W%d" % kin, OWN + c0, OWN + c0 + n), A.min)
            cp(("W%d" % kout, OWN + c0, OWN + c0 + n), ("ci", c0, c0 + n))
            if sums and c0 < L:
                yield
                b = "ps%d" % (4 + c0 // 512)
                o = (b, c0 % 512, c0 % 512 + n)
                r = ("W%d" % kout, OWN + c0, OWN + c0 + n)
                if sums == 1:
                    mm(o, BO, r, True, True)
                else:
                    mm(o, BO, r, True, False)
                    mm(o, N8K, ("p0", c0 + 1, c0 + 1 + n), False, False)
                    mm(o, P8K, ("p0", c0, c0 + n), False, True)
                act(("hp", c0, c0 + n), r, scale=0.5, bias=128.25)
                act(("hb", c0, c0 + n), ("hp", c0, c0 + n), bias=-128.0)
                if sums == 1:
                    act(("g2", c0, c0 + n), ("hp", c0, c0 + n), bias=-384.0)
        return chain

    G1024 = [(0, 256), (256, 256), (512, 256), (768, 192), (960, 64)]
    G1216 = [(1024, 192)] + G1024

    def select_states(P):
        for h in (0, 512):
            ts(("cand", h, h + 512), ("ps%d" % (4 + h // 512), 0, 512), ("thf", 0, 1), A.is_ge)
            ini = 0.0 if h == 0 else T[P][:, 512:513]
            rd = [("cand", h, h + 512), ("c192", h, h + 512)] + ([(P, 512, 513)] if h else [])
            emit("v", lambda h=h, ini=ini: g.vector.tensor_tensor_scan(out=T[P][:, h + 1:h + 513], data0=T.cand[:, h:h + 512], data1=T.c192[:, h:h + 512], initial=ini, op0=A.add, op1=A.min),
                 rd, [(P, h + 1, h + 513)])

    def put_u(k, P, h, bk):
        b = ("ps%d" % bk, 0, 512)
        mm(b, IB, ("W%d" % k, OWN + h, OWN + h + 512), True, False)
        mm(b, N512, (P, h + 1, h + 513), False, False)
        mm(b, P512, (P, h, h + 512), False, True)
        return b

    def find_list(P, bk=(0, 1, 2)):
        b0, b1, b2 = ("ps%d" % bk[0], 0, 64), ("ps%d" % bk[1], 0, 64), ("ps%d" % bk[2], 0, 12)
        for a in range(16):
            mm(b1, col16("cola", a), (P, 0, 1024), a == 0, a == 15, a=a, step=16)
        for a in range(16):
            mm(b0, col16("cola", a), (P, 1, 1025), a == 0, a == 15, a=a, step=16)
        yield
        cp(("lst", 0, 192), ("padj", 0, 192))
        cp(("la", 0, 64), b1)
        tt(("lb", 0, 64), b0, ("la", 0, 64), A.is_equal)
        ts(("lc", 0, 64), b0, 0.0625, A.mult, -1.0, A.add)
        tt(("lb", 0, 64), ("lb", 0, 64), ("cposn", 0, 64), A.mult)
        tt(("lc", 0, 64), ("lc", 0, 64), ("lb", 0, 64), A.add)
        cp(("pos", 0, 64), ("lc", 0, 64))
        yield
        emit("v", lambda: g.vector.tensor_copy(out=T.lst[:, 0:1408].indirect(T.pos[:, 0:64]), in_=T.iotac[:, 0:1024]),
             [("pos", 0, 64), ("iotac", 0, 1024)], [("lst", 0, 1408)])
        cp(("l16", 0, 192), ("lst", 0, 192))
        for a in range(16):
            mm(b2, col16("cola", a), ("l16", 0, 192), a == 0, a == 15, a=a, step=16)
        yield
        ts(("slist", 0, 12), b2, 0.0625, A.mult)

    SL = ("slist", 0, 12)

    def cut(r, k, pb=3):
        gat("v", ("old", 0, 192), ("ef", 0, 1216), SL)
        ts(("offo", 0, 192), ("old", 0, 192), float(NA), A.add)
        for x, e in ((0, "v"), (48, "s" if r == 0 else "v"), (96, "v"), (144, "s" if r == 0 else "v")):
            gb = landing(48)
            gat(e, gb, ("W%d" % k, 0, WW), ("offo", x, x + 48))
            for i in range(16):
                mm(("ps%d" % pb, x, x + 48), col16("pfx", i), gb, i == 0, i == 15, a=i, step=16)
        yield
        ts(("beh", 0, 192), ("ps%d" % pb, 0, 192), ("pf", 8, 9), A.is_ge)
        hr = (L + CAP) + CAP * r
        tt(("ef", hr, hr + 192), ("old", 0, 192), ("beh", 0, 192), A.mult)
        emit("v", lambda: g.vector.tensor_tensor(out=T.ef[:, 0:1216].indirect(T.slist[:, 0:12]), in0=T.old[:, 0:192], in1=T.ef[:, hr:hr + 192], op=A.subtract),
             [SL, ("old", 0, 192), ("ef", hr, hr + 192)], [("ef", 0, 1216)])

    def ecol(c):
        return c if c < L else c + CAP

    def new_off(c0, n):
        ts(("off", c0, c0 + n), ("ef", ecol(c0), ecol(c0) + n), float(NA), A.add)

    run_pass(0, G1024, clip_piece, clip_chain(0, 1, 0), 2 * 1024, 0)
    shown(1)
    for k in range(1, 7):
        if k in (1, 2, 6):
            zero(("W%d" % k, OWN + L, WW))
            zero_halves(k)
        else:
            zero(("W%d" % k, OWN + L + CAP, WW))
    iota(("c192", 0, 1024), [[0, 1024]], 192, 0)
    select_g("cola", A.is_equal, 0.0)
    consts()
    run_pass(1, G1024, clip_piece, clip_chain(1, 2, 1), 2 * 1024, 3 * 1024)
    select_states("p0")
    shown(2, e0="s")
    us = [put_u(2, "p0", h, 6 + h // 512) for h in (0, 512)]
    for h in (0, 512):
        tt(("W3", OWN + h, OWN + h + 512), us[h // 512], ("g2", h, h + 512), A.max)
    gat("s", ("hs", 0, 448), ("hb", 0, L), ("shm", 0, 28))
    fl = find_list("p0")
    next(fl)
    gat("s", ("an", 0, 448), ("W3", NA, OWN + L), ("shl", 0, 28), func=F.Relu, scale=-1.0)
    for i in range(7):
        gat("s", ("snd3", 128 * i, 128 * i + 64), ("W3", NA, OWN + L), ("shl", 4 * i, 4 * i + 4))
    next(fl)
    for i in range(7):
        if i == nfar:
            next(fl)
        tt(("snd3", 128 * i + 64, 128 * i + 128), ("hs", 64 * i, 64 * i + 64), ("an", 64 * i, 64 * i + 64), A.min)
    exchange(3)
    iota(("hm", 0, NA), [[1, NA]], 64 - NA, 0)
    iota(("hm", NA, 2120), [[0, 2120 - NA]], 0, 0)
    act(("xa", 0, L), ("W3", OWN, OWN + L), func=F.Abs, bias=128.0)
    act(("xp", 0, L), ("xa", 0, L), func=F.Abs, bias=128.0, scale=-1.0)
    for _ in fl:
        pass
    gat("s", ("W3", OWN + L, OWN + L + CAP), ("hb", 0, L + CAP), SL)
    for _ in cut(0, 2):
        pass
    new_off(L, CAP)
    act(("xp", L, L + CAP), ("W3", OWN + L, OWN + L + CAP))

    def half_list():
        new_off(0, 256)
        yield
        yield
        yield
        emit("v", lambda: g.vector.tensor_scalar(out=T.hm[:, OWN:2120].indirect(T.slist[:, 0:12]), in0=T.padj[:, 0:192], scalar1=1.0, scalar2=8.0, op0=A.mult, op1=A.add),
             [SL, ("padj", 0, 192)], [("hm", OWN, 2120)])
        yield
        gat("v", ("hg", 0, 448), ("hm", NA, 2120), ("shl", 0, 28))
        for a in range(16):
            mm(("ps7", 0, 28), col16("cola", a), ("hg", 0, 448), a == 0, a == 15, a=a, step=16)
        yield
        yield
        yield
        for i in range(7):
            ts(("sh56", 8 * i + 4, 8 * i + 8), ("ps7", 4 * i, 4 * i + 4), 0.0625, A.mult)

    def first_empty(c0, n):
        ec = ecol(c0)
        ts(("em", c0, c0 + n), ("ef", ec, ec + n), 0.0, A.is_equal, -4096.0, A.mult)
        mm(("ps6", 0, n), TRI, ("em", c0, c0 + n), True, True)
        act(("fe", c0, c0 + n), ("ps6", 0, n), func=F.Relu, scale=-1.0 / 4096)

    GF = [(1024, 192), (0, 256), (256, 256), (512, 256), (768, 256)]

    def fuse_piece(gi, c0, x, gb):
        out = ("ps%d" % (gi % 3), x, x + NP)
        for i in range(16):
            mm(out, col16("lf", i), gb, i == 0, i == 15, a=i, step=16)

    def fuse_chain(gi, c0, n):
        rb, ub, tb, zb = "ps%d" % (gi % 3), "ps%d" % (3 + gi % 2), "ps%d" % (5 + 2 * (gi % 2)), "ps6"
        c1 = c0 + n
        ec = ecol(c0)
        if 0 < gi < len(GF) - 1:
            new_off(*GF[gi + 1])
        if gi == 0:
            yield
        first_empty(c0, n)
        yield
        ts(("k8", c0, c1), (rb, 0, n), MAGIC8, A.add, MAGIC8, A.subtract)
        tt(("ff", c0, c1), (rb, 0, n), ("k8", c0, c1), A.is_lt)
        mm((ub, 0, n), TRI, ("ff", c0, c1), True, False)
        mm((ub, 0, n), BO, ("fe", c0, c1), False, False)
        mm((ub, 0, n), IB, ("cm1", 0, n), False, True)
        for _ in range(YA):
            yield
        act((ub, 0, n), (ub, 0, n), func=F.Relu)
        for _ in range(Y1):
            yield
        tt(("fx", c0, c1), (ub, 0, n), ("ef", ec, ec + n), A.mult)
        for a in range(16):
            mm((tb, 0, n // 16), col16("cola", a), ("fx", c0, c1), a == 0, a == 15, a=a, step=16)
        for _ in range(Y2):
            yield
        tl = ("tl", c0 // 16, c1 // 16)
        ts(tl, (tb, 0, n // 16), float(NA), A.add)
        gat("s", ("ab", c0, c1), ("W3", 0, WW), tl, func=F.Abs, bias=128.0)
        for _ in range(Y3):
            yield
        mm((zb, 0, n), IB, ("cb2", 0, n), True, False)
        mm((zb, 0, n), B32, ("ff", c0, c1), False, False)
        mm((zb, 0, n), NI8, ("ab", c0, c1), False, True)
        tt((zb, 0, n), (zb, 0, n), ("k8", c0, c1), A.add)
        tt(("ci", c0, c1), (zb, 0, n), ("xp", c0, c1), A.min)
        cp(("W4", OWN + c0, OWN + c1), ("ci", c0, c1))

    run_pass(3, GF, fuse_piece, fuse_chain, 10 * 1216, 5 * 1216, 0, bg=[half_list()])
    shown(4, "sh56", 8)

    def insert(c0, n):
        c1, ec = c0 + n, ecol(c0)
        emit("v", lambda: g.vector.tensor_tensor(out=T.tin[:, c0:c1], in0=T.hm[:, 0:2120].indirect(T.tl[:, c0 // 16:c1 // 16]), in1=T.fe[:, c0:c1], op=A.mult),
             [("hm", 0, 2120), ("tl", c0 // 16, c1 // 16), ("fe", c0, c1)], [("tin", c0, c1)])
        tt(("ef", ec, ec + n), ("ef", ec, ec + n), ("tin", c0, c1), A.add)
        new_off(c0, n)

    for c0, n in G1216[:3]:
        insert(c0, n)

    run_pass(4, G1216, clip_piece, clip_chain(4, 5, 2, lambda gi: insert(*G1216[gi + 2]) if 0 < gi < 4 else None), 6 * 1216, 1.7 * 1216, 2)
    select_states("p1")
    for h in (0, 512):
        b = ("ps%d" % (6 + h // 512), 0, 512)
        mm(b, IB, ("p1", h + 1, h + 513), True, False)
        mm(b, NIB, ("p1", h, h + 512), False, True)
        act(("sfl", h, h + 512), b, scale=("pf", 6, 7))
    shown(5, "sh56", 8, send=False)
    shown(6, "shm", 4, srcreg=("sfl", 0, L))
    exchange(5)
    fl = find_list("p1", (4, 5, 4))
    next(fl)
    ts(("cw", 0, L), ("p1", 1, L + 1), ("pf", 4, 5), A.mult, ("pf", 5, 6), A.add)
    for h in (0, 512):
        tt(("W6", OWN + h, OWN + h + 512), ("ps%d" % (6 + h // 512), 0, 512), ("cw", h, h + 512), A.mult)

    def split_beside():
        for _ in fl:
            yield
        yield
        for _ in cut(1, 5, 5):
            yield
        ready.append(1)
        yield
        yield
        gat("s", ("xp", L + CAP, V), ("hb", 0, L + CAP), SL)
        for h in (0, 512):
            b = put_u(5, "p1", h, 6)
            tt(("xp", h, h + 512), b, ("hb", h, h + 512), A.max)
            yield
        emit("y", lambda: g.sync.dma_start(out=T.yv[:, 0:L], in_=T.xp[:, 0:L]), [("xp", 0, L)], [], ("stv", 16))
        emit("y", lambda: g.sync.dma_start(out=T.yv[:, L:L + CAP], in_=T.W5[:, OWN + L:OWN + L + CAP]), [("W5", OWN + L, OWN + L + CAP)], [], ("stv", 32))
        emit("y", lambda: g.sync.dma_start(out=T.yv[:, L + CAP:V], in_=T.xp[:, L + CAP:V]), [("xp", L + CAP, V)], [], ("stv", 48))

    nst = [0]

    def last_piece(gi, c0, x, gb):
        out = ("ps%d" % (gi % 4), x, x + NP)
        for i in range(16):
            mm(out, col16("cola", i), gb, i == 0, i == 15, a=i, step=16)

    def last_chain(gi, c0, n):
        db, ub, xb = "ps%d" % (gi % 4), "ps%d" % (4 + 3 * (gi % 2)), "ps5"
        c1 = c0 + n
        ec = ecol(c0)
        E = ("ef", ec, ec + n)
        yield
        while not ready:
            yield
        first_empty(c0, n)
        act(("nm", c0, c1), E, func=F.Relu, scale=-1.0)
        act(("zz", c0, c1), E, func=F.Sign, bias=-0.5)
        yield
        tt(("ff", c0, c1), (db, 0, n), ("em", c0, c1), A.is_lt)
        tt(("nc", c0, c1), (db, 0, n), ("nm", c0, c1), A.subtract)
        mm((ub, 0, n), TRI, ("ff", c0, c1), True, True)
        for _ in range(X1):
            yield
        act((ub, 0, n), (ub, 0, n), func=F.Relu)
        for _ in range(X2):
            yield
        tt(("fx", c0, c1), (ub, 0, n), ("nc", c0, c1), A.mult)
        mm((xb, 0, n), IB, ("cb3", 0, n), True, False)
        mm((xb, 0, n), N4K, ("fe", c0, c1), False, False)
        mm((xb, 0, n), BO, ("fx", c0, c1), False, True)
        act((xb, 256, 256 + n), ("zz", c0, c1), scale=-1156.0, bias=1148.0)
        for _ in range(X3):
            yield
        tt(("et", c0, c1), E, (xb, 256, 256 + n), A.add)
        tt(("yeb", c0, c1), (xb, 0, n), ("et", c0, c1), A.min)
        nst[0] += 16
        emit("y", lambda: g.sync.dma_start(out=T.ye[:, c0:c1], in_=T.yeb[:, c0:c1]), [("yeb", c0, c1)], [], ("sty", nst[0]))

    GL = [(0, 256), (256, 256), (512, 256), (1024, 192), (768, 128), (1216, 192), (896, 128)]
    run_pass(6, GL, last_piece, last_chain, 7 * 1408, 5 * 1408, 2, bg=[split_beside()], v0=6000.0)

    g.sync.wait_ge(T.sem.sty, nst[0])
    g.sync.wait_ge(T.sem.stv, 48)
    for e in ("v", "s", "t", "g"):
        g.sync.wait_ge(T.sem[SEM[e]], cnt[e])
    g.wait_ge(T.sem.lsem, lsum[0])
